import numpy as np, ml_dtypes
CORES = [40,64,80,88,96,104,120,144]
N = 8
BF = ml_dtypes.bfloat16
def gentries(a):
    return np.ascontiguousarray(a.reshape(8, 16, -1).transpose(0, 2, 1)).reshape(8, -1)
def gtable(e):
    e = np.asarray(e); return np.ascontiguousarray(e.reshape(8, -1, 16).transpose(0, 2, 1)).reshape(128, -1).astype(np.int32)
def f(rng, *shape):
    return (rng.standard_normal(shape, dtype=np.float32) * np.exp2(rng.integers(-2, 3, shape[:-1] + (1,)))).astype(BF)
def wide(rng, *shape):
    v = f(rng, *shape).astype(np.float32); k = shape[:-2] + (1, shape[-1])
    return (v * np.exp2(rng.integers(-6, 7, k)) * (rng.random(k) > 0.0625)).astype(BF)
V, D, C, R = 2048, 3, 32, 2
def ranks(t):
    return t.reshape(8, D, N, V).transpose(2, 0, 1, 3)
def globe(a, bl):
    out = np.zeros((N, 8, D * V), np.int64)
    for r in range(N):
        own = np.broadcast_to(r * V + np.arange(V), (8, V))
        ghosts = (np.arange(N)[:, None, None] * V + bl[:, :, r]).transpose(1, 0, 2).reshape(8, N * C)
        out[r] = np.take_along_axis(np.concatenate([own, ghosts], 1), a[r].reshape(8, D * V).astype(np.int64), 1)
    return out.reshape(N, 8, D, V).transpose(1, 2, 0, 3).reshape(8, D, N * V)
def unpack(nb, bl):
    return np.stack([gentries(t) for t in nb]).reshape(N, 8, D, V), np.stack([gentries(t) for t in bl]).reshape(N, 8, N, C)
def pack(rng, a, bl, v):
    o = np.argsort(rng.random(a.shape), 2); a = np.take_along_axis(a, o, 2); v = np.take_along_axis(v, o, 2)
    return {"nb": np.stack([gtable(t.reshape(8, D * V)) for t in a]), "bl": np.stack([gtable(t.reshape(8, N * C)) for t in bl]),
            "w": np.ascontiguousarray(v).reshape(N, 8, D * V).astype(np.float32).astype(BF), "x": f(rng, N, 128, V)}
def graphs(rng, p):
    bl = np.argsort(rng.random((N, 8, N, V)), axis=-1)[..., :C]
    a = np.full((N, 8, D, V), -1, np.int64)
    for g in range(8):
        for d in range(D):
            for r in range(N):
                for q in range(r):
                    o = rng.permutation(C); u = bl[r, g, q]; t = bl[q, g, r][o]
                    k = (a[r, g, d, u] < 0) & (a[q, g, d, t] < 0) & (rng.random(C) < p)
                    a[r, g, d, u[k]] = V + q * C + o[k]; a[q, g, d, t[k]] = V + r * C + np.flatnonzero(k)
            for r in range(N):
                e = rng.permutation(np.flatnonzero(a[r, g, d] < 0)); h = len(e) // 2
                a[r, g, d, e[:h]] = e[h:2 * h]; a[r, g, d, e[h:2 * h]] = e[:h]
                if len(e) > 2 * h: a[r, g, d, e[-1]] = (e[-1] + 1) % V
        for r in range(N):
            alias = np.full(V, -1, np.int64); alias[bl[r, g, r]] = V + r * C + np.arange(C)
            b = a[r, g]; n = np.where(b < V, alias[np.minimum(b, V - 1)], -1)
            a[r, g] = np.where((n >= 0) & (rng.random((D, V)) < 0.5), n, b)
    return a, bl
def both(a, bl, z):
    return np.array(ranks(np.take_along_axis(z, np.minimum(globe(a, bl), np.arange(N * V)), 2)))
def setup_inputs(rng):
    a, bl = graphs(rng, 0.6)
    return pack(rng, a, bl, both(a, bl, np.exp2(4 * rng.random((8, D, N * V)))))
def setup_inputs_ties(rng):
    a, bl = graphs(rng, 0.6); z = rng.integers(1, 4, (8, D, N * V)).astype(np.float64); z[rng.integers(0, 8)] = 1
    z *= np.exp2(rng.integers(-20, 21, (8, 1, 1)))
    return pack(rng, a, bl, both(a, bl, z))
def setup_inputs_borders(rng):
    a, bl = graphs(rng, 1.0); v = both(a, bl, np.exp2(3 * rng.random((8, D, N * V))))
    far = ranks(globe(a, bl) // V != np.arange(N * V) // V)
    return pack(rng, a, bl, v * np.where(far, 8, 1))
def setup_inputs_hubs(rng):
    a, bl = graphs(rng, 0.6); v = both(a, bl, np.exp2(4 * rng.random((8, D, N * V))))
    for r in range(N):
        for g in range(8):
            e = rng.permutation(V); h = e[:16]; leaves = e[16:V // 2]; b = a[r, g]; c = v[r, g]
            b[:, leaves] = h[rng.integers(0, 16, (D, len(leaves)))]
            b[0, h] = h[np.arange(16) ^ 1]; c[0, h] = 256
    return pack(rng, a, bl, v)
def setup_inputs_any(rng):
    bl = rng.integers(0, V, (N, 8, N, C)); bl[..., C // 2:] = bl[..., :1]; bl[..., 1] = 0; bl[..., 2] = V - 1
    a = rng.integers(0, V + N * C, (N, 8, D, V)); j = np.arange(V)
    a = np.where(ranks(globe(a, bl) == np.arange(N * V)), (j + 1) % V, a)
    o = rng.permutation(8); a[:, o[0]] = (j + 1) % V; a[:, o[1]] = j ^ 1
    for r in range(N):
        for g in o[2:5]:
            q = r ^ 1
            a[r, g, :, bl[r, g, q, 0]] = V + q * C + rng.choice(np.r_[0, C // 2:C], D)
    return pack(rng, a, bl, np.exp2(4 * rng.random((N, 8, D, V))))
def setup_inputs_spread(rng):
    a, bl = graphs(rng, 0.6); z = np.exp2(rng.integers(-3, 4, (8, D, N * V)) + rng.random((8, D, N * V)))
    d = pack(rng, a, bl, both(a, bl, z)); d["x"] = wide(rng, N, 128, V); return d
def check_inputs(d):
    bad = []
    if d["bl"].min() < 0 or d["bl"].max() >= V: bad.append("bl")
    if d["nb"].min() < 0 or d["nb"].max() >= V + N * C: bad.append("nb")
    if not bad and (globe(*unpack(d["nb"], d["bl"])) == np.arange(N * V)).any(): bad.append("own neighbour")
    u = d["w"].astype(np.float32)
    if not (np.isfinite(u).all() and (u > 0).all()): bad.append("w")
    v = np.abs(d["x"].astype(np.float32))
    if not np.isfinite(v).all(): bad.append("x")
    if not 4.0 * D * float(u.max()) * float(v.max()) < 2.0 ** 127: bad.append("range")
    return bad
def reference(nb, bl, w, x):
    i = np.arange(N * V); A = globe(*unpack(nb, bl))
    u = w.astype(np.float64).reshape(N, 8, D, V).transpose(1, 2, 0, 3).reshape(8, D, N * V)
    mate = np.tile(i, (8, 1)); free = np.ones((8, N * V), bool)
    for t in range(R):
        k = np.where(np.take_along_axis(free[:, None], A, 2), u, 0.0)
        P = np.take_along_axis(A, np.argmax(k, 1)[:, None], 1)[:, 0]
        P = np.where(free & (np.max(k, 1) > 0), P, -1)
        hit = (P >= 0) & (np.take_along_axis(P, np.maximum(P, 0), 1) == i)
        mate = np.where(hit, P, mate); free = free & ~hit
    two = mate != i; first = np.minimum(mate, i); rep = first == i
    num = (np.add.accumulate(rep.reshape(8, N, V).astype(np.int64), 2) - 1 + V * np.arange(N)[:, None]).reshape(8, N * V)
    cm = np.take_along_axis(num, first, 1).reshape(8, N, V)
    xx = np.ascontiguousarray(x.astype(np.float64).reshape(N, 8, 16, V).transpose(1, 2, 0, 3)).reshape(8, 16, N * V)
    X = xx + np.where(two[:, None], np.take_along_axis(xx, mate[:, None], 2), 0.0)
    s = np.zeros((8, 16, N * V))
    for d in range(D):
        s += u[:, d, None] * np.take_along_axis(X, A[:, d, None], 2)
    s = s + np.where(two[:, None], np.take_along_axis(s, mate[:, None], 2), 0.0)
    y = np.zeros((8, 16, N * V))
    for g in range(8):
        y[g][:, num[g, rep[g]]] = s[g][:, rep[g]]
    y = np.ascontiguousarray(y.reshape(8, 16, N, V).transpose(2, 0, 1, 3)).reshape(N, 128, V)
    return {"y": y.astype(np.float32), "cm": np.stack([gtable(cm[:, r]) for r in range(N)]).astype(np.float32)}

@@ -1,0 +1,529 @@
+from concourse.mybir import AluOpType, ActivationFunctionType
+from concourse.bass import DstId, RemoteDMATransfer
+
+N, V, C, D = 8, 2048, 32, 3
+GH, NONE = V, V + N * C
+EXT = NONE + 16
+
+
+def buffers(*groups):
+    out = {}
+    for names, width, dtype in groups:
+        for n in names.split():
+            out[n] = ("sbuf", [128, width], dtype)
+    return out
+
+
+SCRATCH = buffers(
+    ("bli gl bsh", 16, "int32"), ("nbi", 384, "int32"), ("pi", 8, "int32"), ("gbi", 256, "int32"), ("r0", 2, "int32"),
+    ("wa tr", 384, "bfloat16"), ("wb", 6144, "bfloat16"), ("s0 s1", 160, "bfloat16"), ("e1 ehl", 144, "bfloat16"),
+    ("gn go nt rep", 128, "bfloat16"), ("xe hl m1 nx", EXT, "bfloat16"), ("lo", NONE, "bfloat16"),
+    ("xb m1b nxb", 256, "bfloat16"), ("fb", 1024, "bfloat16"), ("f1 f2 f3 mm hg cg x2", V, "bfloat16"),
+    ("lw", 2 * V, "bfloat16"), ("rX r2 r6", C, "bfloat16"),
+    ("blo glo pcb", 16, "uint16"), ("boff", 48, "uint16"), ("bpo", 64, "uint16"), ("pco mo lam no rhoo l1", 128, "uint16"),
+    ("nbo po", 384, "uint16"),
+    ("pc ub qb", 16, "float32"), ("r1 r3 r4 r5", C, "float32"), ("bp db", 48, "float32"), ("xi", 160, "float32"),
+    ("eall", 144, "float32"), ("gm ones va va2 w1s g1 g2 wm wl dn ta tb tc td te", 128, "float32"),
+    ("qa ua pcf gt pz mt nr lt inc nn rho rn cmf", 128, "float32"), ("nbf pa da", 384, "float32"),
+    ("qc gbb bmask t1b t2b xcb mb xm xxb sb", 256, "float32"), ("pg", 768, "float32"), ("gs", 1024, "float32"),
+    ("rt t1 t2 xx sx", EXT, "float32"), ("p1 p2 p3 yy", V, "float32"), ("sp", V + 8, "float32"))
+PSUM = {"ps": 2048, "a0": 512, "a1": 512, "a2": 512, "a3": 512}
+for _n in PSUM:
+    SCRATCH[_n] = ("psum", [128, PSUM[_n]], "float32")
+EXCH = {"0": ("bli", "gl", 0, 2), "1": ("t1b", "t1", GH, C), "X": ("xb", "xe", GH, C), "2": ("m1b", "m1", GH, C),
+        "3": ("t2b", "t2", GH, C), "4": ("xxb", "xx", GH, C), "6": ("nxb", "nx", GH, C), "5": ("sb", "sx", GH, C)}
+ORDER = ["0", "1", "X", "2", "3", "4", "6", "5"]
+DMAS = ["bl", "gl", "nb", "w0", "w1", "w2", "x", "wb", "lo", "cm", "y0", "y1", "y2", "y3"]
+SEMAPHORES = (["v", "s", "t", "p", "loc", "rloc"] + ["d" + n for n in DMAS] + ["arr" + k for k in ORDER]
+              + ["hop" + k for k in ORDER])
+
+
+def pick(engines, i, n):
+    m = 0
+    for e in engines[i * n:(i + 1) * n]:
+        m |= 1 << e
+    return m
+
+
+def plan(src, T, topo):
+    near, far = [], []
+    for d in T.cores:
+        if d != src:
+            (near if topo.may_write(src, d) else far).append(d)
+    hops = [c for c in topo.cores_of(src) if c != src and all(topo.may_write(c, d) for d in far)]
+    straight = [(d, pick(topo.engines(src, d), i, 2)) for i, d in enumerate(near)]
+    over = []
+    for i, d in enumerate(far):
+        h = hops[i]
+        over.append((h, pick(topo.engines(src, h), i, 4), d, topo.mask(h, d)))
+    return straight, over
+
+
+def bits(m):
+    return bin(m).count("1")
+
+
+def hop_program(g, core, T, topo):
+    for src in topo.cores_of(core):
+        if T.rank_of(src) is None:
+            continue
+        r = T.rank_of(src)
+        for h, m_in, d, m_out in plan(src, T, topo)[1]:
+            if h != core:
+                continue
+            rid, pid = topo.addr(d, core)
+            for k in ORDER:
+                _, land, c0, w = EXCH[k]
+                g.wait_ge(T.sem["hop" + k], bits(m_in))
+                g.remote_dma(T[land][:, c0 + w * r:c0 + w * r + w], T["r" + k][:], T.sem["arr" + k], T.sem.rloc,
+                             pid, rid, m_out)
+            g.wait_ge(T.sem.rloc, bits(m_out) * len(ORDER))
+
+
+def rank_program(g, core, T, topo):
+    rank = T.rank_of(core)
+    if rank is None:
+        hop_program(g, core, T, topo)
+        return
+    A = AluOpType
+    COPY, IDENT = ActivationFunctionType.Copy, ActivationFunctionType.Identity
+    q_of = {"v": g.vector, "s": g.scalar, "t": g.tensor, "g": g, "y": g.sync}
+    count = {"v": 0, "s": 0, "t": 0, "p": 0}
+    waited = {"v": {}, "s": {}, "t": {}, "g": {}, "y": {}}
+    log = {}
+    totals = {}
+
+    def need(queue, tokens):
+        best = {}
+        for s, n in tokens:
+            best[s] = max(n, best.get(s, 0))
+        for s in sorted(best):
+            if waited[queue].get(s, 0) < best[s]:
+                q_of[queue].wait_ge(T.sem[s], best[s])
+                waited[queue][s] = best[s]
+
+    def deps(queue, reads, writes):
+        out = []
+        for regs, wr in ((reads, False), (writes, True)):
+            for name, lo, hi in regs:
+                if name in PSUM:
+                    lo, hi = lo // 512 * 512, -(-hi // 512) * 512
+                for l, h, w, tok, qq in log.get(name, []):
+                    if l < hi and lo < h:
+                        if name in PSUM:
+                            if qq == queue and (queue == "t" or not (w or wr)):
+                                continue
+                            out.append(tok)
+                        elif w or wr:
+                            out.append(tok)
+        return out
+
+    def note(queue, reads, writes, tok):
+        for regs, wr in ((reads, False), (writes, True)):
+            for name, lo, hi in regs:
+                if name in PSUM:
+                    lo, hi = lo // 512 * 512, -(-hi // 512) * 512
+                log.setdefault(name, []).append((lo, hi, wr, tok, queue))
+
+    def ap(r):
+        if r[0] == "ind":
+            return ap(r[1]).indirect(ap(r[2]))
+        name, lo, hi = r[0], r[1], r[2]
+        return T[name][:, lo:hi] if len(r) == 3 else T[name][:, lo:hi:r[3]]
+
+    def regs(rs):
+        out = []
+        for r in rs:
+            if isinstance(r, tuple):
+                if r[0] == "ind":
+                    out += regs([r[1], r[2]])
+                else:
+                    out.append((r[0], r[1], r[2]))
+        return out
+
+    def val(x):
+        return ap(x) if isinstance(x, tuple) else x
+
+    def run(queue, reads, outs, emit):
+        rd, wr = regs(reads), []
+        for o in outs:
+            if o[0] == "ind":
+                wr += regs([o[1]])
+                rd += regs([o[2]])
+            else:
+                wr += regs([o])
+        need(queue, deps(queue, rd, wr))
+        s = "p" if queue == "g" else queue
+        count[s] += 1
+        emit().then_inc(T.sem[s], 1)
+        note(queue, rd, wr, (s, count[s]))
+
+    def tt(out, a, b, op):
+        run("v", [a, b], [out], lambda: g.vector.tensor_tensor(ap(out), ap(a), ap(b), op))
+
+    def ts(out, a, s1, op0, s2=None, op1=None):
+        if op1 is None:
+            run("v", [a, s1], [out], lambda: g.vector.tensor_scalar(ap(out), ap(a), val(s1), None, op0))
+        else:
+            run("v", [a, s1, s2], [out], lambda: g.vector.tensor_scalar(ap(out), ap(a), val(s1), val(s2), op0, op1))
+
+    def cp(out, a):
+        run("v", [a], [out], lambda: g.vector.tensor_copy(ap(out), ap(a)))
+
+    def sc(out, a):
+        run("s", [a], [out], lambda: g.scalar.activation(ap(out), ap(a), COPY))
+
+    def sa(out, a, scale, bias):
+        run("s", [a], [out], lambda: g.scalar.activation(ap(out), ap(a), IDENT, bias=float(bias), scale=float(scale)))
+
+    def fill(out, c):
+        run("v", [], [out], lambda: g.vector.memset(ap(out), c))
+
+    def iota(out, pattern, base, ch):
+        run("g", [], [out], lambda: g.iota(ap(out), pattern, base, ch, allow_small_or_imprecise_dtypes=True))
+
+    def mm(group):
+        rd = regs([m[1] for m in group] + [m[2] for m in group])
+        wr = regs([m[0] for m in group])
+        need("t", deps("t", rd, wr))
+        ins = None
+        for o, l, r, st, sp in group:
+            ins = g.tensor.matmul(ap(o), ap(l), ap(r), st, sp)
+        count["t"] += 1
+        ins.then_inc(T.sem.t, 1)
+        note("t", list(dict.fromkeys(rd)), list(dict.fromkeys(wr)), ("t", count["t"]))
+
+    def to_a(ps, c0, n, lhs, src, base=0):
+        mm([((ps, c0, c0 + n), (lhs, 15 - k, 143 - k), (src, base + k, base + 16 * n, 16), k == 0, k == 15)
+            for k in range(16)])
+
+    def dma(queue, sem, out, in_, reads, writes):
+        need(queue, deps(queue, reads, writes))
+        q_of[queue].dma_start(out, in_).then_inc(T.sem["d" + sem], 16)
+        totals["d" + sem] = totals.get("d" + sem, 0) + 16
+        note(queue, reads, writes, ("d" + sem, totals["d" + sem]))
+
+    straight, over = plan(core, T, topo)
+    sent = [0]
+
+    def send(k):
+        src, land, c0, w = EXCH[k]
+        need("g", deps("g", [(src, 0, w * N)], []))
+
+        def block(d):
+            q = T.rank_of(d)
+            return T[src][:, w * q:w * q + w]
+        calls = []
+        for h, m_in, d, _ in over:
+            rid, pid = topo.addr(h, core)
+            calls.append(RemoteDMATransfer(dst_ids=[DstId(rid=rid, pnc=pid)], dma_engine_mask=m_in, remote_sem=T.sem["hop" + k],
+                                           src=block(d), dst=T["r" + k][:]))
+            sent[0] += bits(m_in)
+        g.remote_dma_fused(calls, local_sem=T.sem.loc)
+        calls = []
+        for d, m in straight:
+            rid, pid = topo.addr(d, core)
+            calls.append(RemoteDMATransfer(dst_ids=[DstId(rid=rid, pnc=pid)], dma_engine_mask=m, remote_sem=T.sem["arr" + k],
+                                           src=block(d), dst=T[land][:, c0 + w * rank:c0 + w * rank + w]))
+            sent[0] += bits(m)
+        g.remote_dma_fused(calls, local_sem=T.sem.loc)
+
+    def arrive(k):
+        n = 0
+        for c in T.cores:
+            if c != core:
+                near, far = plan(c, T, topo)
+                n += sum(bits(m) for d, m in near if d == core) + sum(bits(m) for _, _, d, m in far if d == core)
+        _, land, c0, w = EXCH[k]
+        totals["arr" + k] = n
+        note("net", [], [(land, c0, c0 + w * N)], ("arr" + k, n))
+
+    def alias(copy, land, src):
+        copy((land, GH + C * rank, GH + C * rank + C), (src, C * rank, C * rank + C))
+
+    base = rank * V
+    dma("y", "bl", T.bli[:], T.bl[:], [], [("bli", 0, 16)])
+    for d in range(D):
+        dma("s" if d == 1 else "y", "w%d" % d, T.wa[:, 128 * d:128 * d + 128], T.w[:, V * d:V * d + V], [],
+            [("wa", 128 * d, 128 * d + 128)])
+    dma("s", "nb", T.nbi[:], T.nb[:], [], [("nbi", 0, 384)])
+    dma("y", "gl", T.gl[:, 2 * rank:2 * rank + 2], T.bl[:, 2 * rank:2 * rank + 2], [], [("gl", 2 * rank, 2 * rank + 2)])
+    dma("y", "x", T.xe[:, 0:V], T.x[:], [], [("xe", 0, V)])
+
+    iota(("pi", 0, 1), [[1, 1]], 0, 1)
+    iota(("xi", 0, 160), [[1, 160]], 0, 0)
+    iota(("rt", 0, 512), [[1, 512]], base, 0)
+    send("0")
+    iota(("qc", 0, 256), [[V, N], [0, C]], -base, 0)
+    iota(("gm", 0, 128), [[16, 8], [0, 16]], 0, 0)
+    iota(("va", 0, 128), [[16, 128]], base, 1)
+    iota(("lo", 0, 128), [[1, 128]], 0, 0)
+    iota(("hl", 0, V), [[1, 16], [0, 128]], 16 * rank, 0)
+    iota(("hl", GH, NONE), [[16, N], [0, C]], 0, 0)
+
+    def col(i):
+        return ("pc", i, i + 1)
+
+    def a(name, i=0):
+        return (name, 128 * i, 128 * i + 128)
+    ts(("pi", 2, 3), ("pi", 0, 1), 4, A.arith_shift_right, 1, A.bitwise_and)
+    ts(("pi", 1, 2), ("pi", 0, 1), 15, A.bitwise_and)
+    ts(col(1), ("pi", 0, 1), 16, A.add)
+    cp(col(3), ("pi", 2, 3))
+    ts(col(2), ("pi", 2, 3), -1, A.mult, 1, A.add)
+    ts(("s0", 0, 160), ("xi", 0, 160), col(1), A.is_equal, col(2), A.mult)
+    ts(("s1", 0, 160), ("xi", 0, 160), col(1), A.is_equal, col(3), A.mult)
+    cp(col(4), ("pi", 1, 2))
+    tt(col(5), ("pi", 0, 1), ("pi", 1, 2), A.subtract)
+    for i in range(1, 4):
+        sa(("rt", 512 * i, 512 * i + 512), ("rt", 0, 512), 1, 512 * i)
+    sc(("ps", 0, V), ("rt", 0, V))
+    sa(("lw", 0, V), ("rt", 0, V), 0, -1)
+    sa(("lo", GH, NONE), ("rt", 0, 256), 0, 0)
+    sa(a("ones"), ("rt", 0, 128), 0, 1)
+    run("v", [("wa", 0, 384)], [("tr", 0, 384)], lambda: g.vector.transpose(T.tr[:], T.wa[:]))
+    for d in range(D):
+        grp = []
+        for i in range(8):
+            b, h = i // 2, i % 2
+            for gg in range(2):
+                st = 16 - 16 * (gg - h)
+                grp.append((("a0", 128 * d + i, 128 * d + 128, 8), ("s%d" % h, st, st + 128),
+                            ("tr", 128 * d + 32 * b + 16 * gg, 128 * d + 32 * b + 16 * gg + 16), gg == 0, gg == 1))
+        mm(grp)
+    cp(("nbf", 0, 384), ("nbi", 0, 384))
+    nb = [a("nbf", d) for d in range(D)]
+    tt(a("dn"), nb[1], nb[0], A.subtract)
+    cp(("blo", 0, 16), ("bli", 0, 16))
+    cp(("gbb", 0, 256), ("ind", ("rt", 0, V), ("blo", 0, 16)))
+    ts(("bsh", 0, 16), ("bli", 0, 16), 4, A.arith_shift_right)
+    cp(("gbi", 0, 256), ("gbb", 0, 256))
+    for d in range(D):
+        ts(("boff", 16 * d, 16 * d + 16), ("bsh", 0, 16), 128 * d, A.add)
+    ts(("gbi", 0, 256), ("gbi", 0, 256), 15, A.bitwise_and)
+    ts(col(6), col(5), 15, A.add)
+    ts(("bmask", 0, 256), ("gbi", 0, 256), col(4), A.is_equal)
+    ts(("eall", 0, 143), ("xi", 0, 143), col(6), A.is_equal)
+    fill(("rt", NONE, NONE + 8), -1.0)
+    cp(a("w1s"), a("a0", 1))
+    tt(a("g1"), a("w1s"), a("a0", 0), A.is_gt)
+    tt(a("wm"), a("w1s"), a("a0", 0), A.max)
+    tt(a("ta"), a("g1"), a("dn"), A.mult)
+    tt(a("g2"), a("a0", 2), a("wm"), A.is_gt)
+    tt(a("tb"), a("ta"), nb[0], A.add)
+    tt(a("tc"), nb[2], a("tb"), A.subtract)
+    tt(a("td"), a("g2"), a("tc"), A.mult)
+    tt(a("pa"), a("tb"), a("td"), A.add)
+    cp(a("po"), a("pa"))
+    arrive("0")
+    cp(("glo", 0, 16), ("gl", 0, 16))
+    tt(("rt", GH, NONE), ("ind", ("rt", 0, V), ("glo", 0, 16)), ("qc", 0, 256), A.add)
+    cp(("t1", 0, 1024), ("ind", ("rt", 0, NONE + 8), ("po", 0, 64)))
+    sc(("t1", 1024, V), ("ind", ("rt", 0, NONE + 8), ("po", 64, 128)))
+    cp(("t1b", 0, 256), ("ind", ("t1", 0, V), ("blo", 0, 16)))
+    alias(cp, "t1", "t1b")
+    send("1")
+
+    def border(d):
+        tt(("pg", 256 * d, 256 * d + 256), ("ind", ("pa", 0, 384 if d else 128), ("boff", 16 * d, 16 * d + 16)),
+           ("bmask", 0, 256), A.mult)
+    border(0)
+    to_a("a1", 0, 16, "eall", "pg", 0)
+    sc(("xb", 0, 256), ("ind", ("xe", 0, V), ("blo", 0, 16)))
+    alias(sc, "xe", "xb")
+    send("X")
+    for n in (128, 256, 512, 1024):
+        sc(("lo", n, 2 * n), ("lo", 0, n))
+    tt(a("wl"), a("w1s"), a("a0", 0), A.min)
+    tt(a("te"), nb[0], nb[1], A.add)
+    tt(a("g1"), a("a0", 2), a("wl"), A.is_gt)
+    tt(a("ta"), a("te"), a("tb"), A.subtract)
+    tt(a("te"), a("te"), nb[2], A.add)
+    tt(a("tc"), nb[2], a("ta"), A.subtract)
+    tt(a("te"), a("te"), a("pa"), A.subtract)
+    tt(a("td"), a("g1"), a("tc"), A.mult)
+    tt(a("pa", 2), nb[2], a("td"), A.subtract)
+    tt(a("pa", 1), a("te"), a("pa", 2), A.subtract)
+    border(1)
+    border(2)
+    to_a("a2", 0, 32, "eall", "pg", 256)
+    ts(col(7), col(4), 0, A.is_equal)
+    ts(col(8), col(4), 1, A.is_equal)
+    ts(("e1", 0, 143), ("xi", 0, 143), col(6), A.is_equal, col(7), A.mult)
+    cp(("bpo", 0, 16), ("a1", 0, 16))
+    cp(("bp", 0, 16), ("a1", 0, 16))
+    arrive("1")
+    tt(("m1b", 0, 256), ("ind", ("t1", 0, NONE), ("bpo", 0, 16)), ("gbb", 0, 256), A.is_equal)
+    alias(cp, "m1", "m1b")
+    send("2")
+
+    def mutual(out, tab, lst, width, a0, a1):
+        sc(("gs", 0, 1024), ("ind", (tab, 0, width), (lst, 64, 128)))
+        tt((out, 0, 1024), ("ind", (tab, 0, width), (lst, 0, 64)), ("rt", 0, 1024), A.is_equal)
+        to_a(a0[0], a0[1], 64, "e1", out, 0)
+        tt((out, 1024, V), ("gs", 0, 1024), ("ps", 1024, V), A.is_equal)
+        to_a(a1[0], a1[1], 64, "e1", out, 1024)
+    mutual("m1", "t1", "po", NONE, ("a3", 0), ("a3", 64))
+    sc(("x2", 0, V), ("xe", 0, V))
+    cp(("po", 128, 384), ("pa", 128, 384))
+    dma("y", "lo", T.hl[1::16, 0:NONE], T.lo[1::16, 0:NONE], [("lo", 0, NONE)], [("hl", 0, NONE)])
+    cp(("bpo", 16, 48), ("a2", 0, 32))
+    cp(("bp", 16, 48), ("a2", 0, 32))
+    cp(("bpo", 48, 64), ("blo", 0, 16))
+    for buf, src, n in (("db", "bp", 16), ("da", "pa", 128)):
+        tt((buf, 0, n), (src, n, 2 * n), (src, 0, n), A.subtract)
+        tt((buf, n, 2 * n), (src, 2 * n, 3 * n), (src, n, 2 * n), A.subtract)
+        ts((buf, 2 * n, 3 * n), (src, 2 * n, 3 * n), -1, A.mult, NONE, A.add)
+    ts(a("qa"), a("a3"), -1, A.mult, 1, A.add)
+    tt(a("da", 0), a("da", 0), a("qa"), A.mult)
+    for c in range(16):
+        dma("y", "wb", T.wb[c::16, :], T.w[:], [("m1", 0, V)], [])
+    note("y", [], [("wb", 0, 6144)], ("dwb", totals["dwb"]))
+    ts(a("va"), a("va"), col(5), A.subtract)
+    ts(a("gn"), a("gm"), col(5), A.is_equal)
+    ts(col(9), col(7), 128, A.mult)
+    ts(a("va2"), a("va"), V - base, A.add)
+    tt(col(10), col(8), col(9), A.add)
+    sa(a("go"), a("gn"), -1, 0)
+    ts(("ehl", 0, 143), ("xi", 0, 143), col(6), A.is_equal, col(10), A.mult)
+    fill(("t2", NONE, NONE + 8), -1.0)
+    fill(("xe", NONE, EXT), 0.0)
+    fill(("nx", NONE, EXT), 0.0)
+    fill(("sx", NONE, NONE + 8), 0.0)
+    fill(("sp", 0, 8), 0.0)
+    fill(("hl", NONE, EXT), 0.0)
+    arrive("2")
+    fl = ("m1", 0, NONE)
+    sc(("fb", 0, 1024), ("ind", fl, ("bpo", 0, 64)))
+    to_a("a0", 0, 64, "e1", "fb")
+
+    def flags(eng, f, d, h):
+        eng((f, 1024 * h, 1024 * h + 1024), ("ind", fl, ("po", 128 * d + 64 * h, 128 * d + 64 * h + 64)))
+
+    def ps16(i):
+        return ("a0", 16 * i, 16 * i + 16)
+
+    def b16(n, i):
+        return (n, 16 * i, 16 * i + 16)
+    ub, ua = ("ub", 0, 16), a("ua")
+    flags(cp, "f3", 2, 0)
+    flags(sc, "f1", 0, 0)
+    to_a("a1", 0, 64, "e1", "f3", 0)
+    flags(cp, "f3", 2, 1)
+    to_a("a1", 64, 64, "e1", "f3", 1024)
+    flags(sc, "f1", 0, 1)
+    to_a("a3", 0, 64, "e1", "f1", 0)
+    flags(cp, "f2", 1, 0)
+    ts(("qb", 0, 16), ps16(3), -1, A.mult, 1, A.add)
+    tt(ub, ps16(2), b16("db", 2), A.mult)
+    tt(ub, ub, b16("db", 1), A.add)
+    tt(ub, ub, ps16(1), A.mult)
+    tt(ub, ub, b16("db", 0), A.add)
+    tt(ub, ub, ps16(0), A.mult)
+    tt(ub, ub, ("qb", 0, 16), A.mult)
+    tt(ub, ub, b16("bp", 0), A.add)
+    cp(("pcb", 0, 16), ub)
+    sc(("t2b", 0, 256), ("ind", ("rt", 0, NONE + 8), ("pcb", 0, 16)))
+    alias(sc, "t2", "t2b")
+    send("3")
+    run("g", [a("go")], [a("nt")], lambda: g.affine_select(T.nt[:], T.go[:], [[-1, 128]], A.is_ge, 0.0, 0, 1))
+    to_a("a2", 0, 64, "e1", "f2", 0)
+    to_a("a3", 64, 64, "e1", "f1", 1024)
+    flags(cp, "f2", 1, 1)
+    to_a("a2", 64, 64, "e1", "f2", 1024)
+    tt(ua, a("a1"), a("da", 2), A.mult)
+    tt(ua, ua, a("da", 1), A.add)
+    tt(ua, ua, a("qa"), A.mult)
+    tt(ua, ua, a("a2"), A.mult)
+    tt(ua, ua, a("da", 0), A.add)
+    tt(ua, ua, a("a3"), A.mult)
+    tt(a("pcf"), ua, a("pa"), A.add)
+    cp(a("pco"), a("pcf"))
+    full = ("rt", 0, NONE + 8)
+    cp(("t2", 0, 1024), ("ind", full, ("pco", 0, 64)))
+    sc(("t2", 1024, V), ("ind", full, ("pco", 64, 128)))
+    arrive("X")
+    sc(("xcb", 0, 256), ("ind", ("xe", 0, EXT), ("pcb", 0, 16)))
+    sc(("a1", 0, 256), ("xcb", 0, 256))
+    sc(("a1", 256, 512), ("xb", 0, 256))
+    ts(a("pz"), a("pcf"), -NONE, A.add)
+    cp(("hl", GH + C * rank, GH + C * rank + C), ("ind", ("hl", 0, V), ("blo", 2 * rank, 2 * rank + 2)))
+    arrive("3")
+    tt(("mb", 0, 256), ("ind", ("t2", 0, NONE + 8), ("pcb", 0, 16)), ("gbb", 0, 256), A.is_equal)
+    tt(("xm", 0, 256), ("mb", 0, 256), ("a1", 0, 256), A.mult)
+    tt(("xxb", 0, 256), ("xm", 0, 256), ("a1", 256, 512), A.add)
+    send("4")
+    mutual("mm", "t2", "pco", NONE + 8, ("a0", 0), ("a2", 0))
+    alias(sc, "xx", "xxb")
+    sc(("hg", 0, V), ("ind", ("hl", 0, EXT), ("pco", 0, 128)))
+    to_a("a3", 0, 128, "ehl", "hg")
+    for h, ma in ((0, ("a0", 0, 64)), (1, ("a2", 0, 64))):
+        c0, c1 = 64 * h, 64 * h + 64
+        tt(("mt", c0, c1), ("pz", c0, c1), ma, A.mult)
+        ts(("mo", c0, c1), ("mt", c0, c1), NONE, A.add)
+        tt(("xx", 1024 * h, 1024 * h + 1024), ("ind", ("xe", 0, EXT), ("mo", c0, c1)), ("x2", 1024 * h, 1024 * h + 1024), A.add)
+    tt(a("gt"), a("a3"), a("va"), A.is_gt)
+    tt(("rep", 0, 64), ("gt", 0, 64), ("a0", 0, 64), A.is_ge)
+    tt(("rep", 64, 128), ("gt", 64, 128), ("a2", 0, 64), A.is_ge)
+    mm([(a("a1"), a("gn"), a("rep"), True, True)])
+    mm([(a("a3"), a("nt"), a("rep"), True, True)])
+    ts(("nbo", 0, 384), ("nbf", 0, 384), 0, A.add)
+    ts(a("nr"), a("rep"), -1, A.mult, 1, A.add)
+    run("v", [a("ones"), a("a1")], [a("inc")],
+        lambda: g.vector.tensor_tensor_scan(T.inc[:], T.ones[:], T.a1[:, 0:128], 0.0, A.mult, A.add))
+    tt(a("nn"), a("inc"), a("a3"), A.add)
+    arrive("4")
+
+    def prod(buf, d, h):
+        tt((buf, 1024 * h, 1024 * h + 1024), ("ind", ("xx", 0, NONE), ("nbo", 128 * d + 64 * h, 128 * d + 64 * h + 64)),
+           ("wb", V * d + 1024 * h, V * d + 1024 * h + 1024), A.mult)
+
+    def half(buf, h):
+        return (buf, 1024 * h, 1024 * h + 1024)
+    for i in range(4):
+        sc(("a%d" % i, 0, 512), ("wb", 2 * V + 512 * i, 2 * V + 512 * i + 512))
+    for h in range(2):
+        sc(half("p3", h), ("ind", ("xx", 0, NONE), ("nbo", 256 + 64 * h, 320 + 64 * h)))
+        prod("p1", 0, h)
+        sc(half("ps", h), half("p1", h))
+    cp(a("no"), a("nn"))
+    tt(a("lt"), a("pz"), a("nr"), A.mult)
+    tt(a("rho"), a("va2"), a("nn"), A.subtract)
+    ts(a("lam"), a("lt"), NONE, A.add)
+    tt(a("rho"), a("rho"), a("nr"), A.mult)
+    ts(a("rn"), a("nn"), base, A.add)
+    tt(a("rho"), a("rho"), a("nn"), A.add)
+    tt(a("rn"), a("rn"), a("rep"), A.mult)
+    cp(a("rhoo"), a("rho"))
+    sc(("nx", 0, V), ("ind", ("hl", 0, V), ("no", 0, 128)))
+    sc(("nxb", 0, 256), ("ind", ("nx", 0, V), ("blo", 0, 16)))
+    alias(sc, "nx", "nxb")
+    send("6")
+    for h in range(2):
+        prod("p2", 1, h)
+        tt(half("ps", h), half("p2", h), half("ps", h), A.add)
+    for h in range(2):
+        for i in (2 * h, 2 * h + 1):
+            c = (512 * i, 512 * i + 512)
+            tt(("p2",) + c, ("p3",) + c, ("a%d" % i, 0, 512), A.mult)
+        tt(half("sx", h), half("p2", h), half("ps", h), A.add)
+        sc(half("p3", h), half("sx", h))
+    cp(("sb", 0, 256), ("ind", ("sx", 0, V), ("blo", 0, 16)))
+    alias(cp, "sx", "sb")
+    send("5")
+    run("v", [("hl", 0, V)], [("ind", ("lw", 0, 2 * V), ("rhoo", 0, 128))],
+        lambda: g.vector.tensor_copy(ap(("ind", ("lw", 0, 2 * V), ("rhoo", 0, 128))), T.hl[:, 0:V]))
+    to_a("a3", 0, 128, "ehl", "lw")
+    arrive("6")
+    sc(("cg", 0, V), ("ind", ("nx", 0, EXT), ("lam", 0, 128)))
+    to_a("a1", 0, 128, "ehl", "cg")
+    arrive("5")
+    tt(("sp", 8, V + 8), ("ind", ("sx", 0, NONE + 8), ("mo", 0, 128)), ("p3", 0, V), A.add)
+    ts(a("l1"), a("a3"), 8 - base, A.add, 0, A.max)
+    for i, eng in ((0, cp), (2, sc), (1, cp), (3, sc)):
+        eng(("yy", 512 * i, 512 * i + 512), ("ind", ("sp", 0, V + 8), ("l1", 32 * i, 32 * i + 32)))
+    for i in (0, 2, 1, 3):
+        dma("y", "y%d" % i, T.y[:, 512 * i:512 * i + 512], T.yy[:, 512 * i:512 * i + 512], [("yy", 512 * i, 512 * i + 512)], [])
+    tt(a("cmf"), a("rn"), a("a1"), A.add)
+    dma("y", "cm", T.cm[:], T.cmf[:], [a("cmf")], [])
+    need("g", [("loc", sent[0])] + [(s, count[s]) for s in ("v", "s", "t", "p")] + sorted(totals.items()))

@@ -15,25 +15,25 @@ def buffers(*groups):
 
 
 SCRATCH = buffers(
-    ("bli gl bsh", 16, "int32"), ("nbi", 384, "int32"), ("pi", 8, "int32"), ("gbi", 256, "int32"), ("r0", 2, "int32"),
+    ("bli bsh bms", 16, "int32"), ("nbi", 384, "int32"), ("pi", 8, "int32"),
     ("wa tr", 384, "bfloat16"), ("wb", 6144, "bfloat16"), ("s0 s1", 160, "bfloat16"), ("e1 ehl", 144, "bfloat16"),
     ("gn go nt rep", 128, "bfloat16"), ("xe hl m1 nx", EXT, "bfloat16"), ("lo", NONE, "bfloat16"),
     ("xb m1b nxb", 256, "bfloat16"), ("fb", 1024, "bfloat16"), ("f1 f2 f3 mm hg cg x2", V, "bfloat16"),
     ("lw", 2 * V, "bfloat16"), ("rX r2 r6", C, "bfloat16"),
-    ("blo glo pcb", 16, "uint16"), ("boff", 48, "uint16"), ("bpo", 64, "uint16"), ("pco mo lam no rhoo l1", 128, "uint16"),
-    ("nbo po", 384, "uint16"),
-    ("pc ub qb", 16, "float32"), ("r1 r3 r4 r5", C, "float32"), ("bp db", 48, "float32"), ("xi", 160, "float32"),
-    ("eall", 144, "float32"), ("gm ones va va2 w1s g1 g2 wm wl dn ta tb tc td te", 128, "float32"),
-    ("qa ua pcf gt pz mt nr lt inc nn rho rn cmf", 128, "float32"), ("nbf pa da", 384, "float32"),
-    ("qc gbb bmask t1b t2b xcb mb xm xxb sb", 256, "float32"), ("pg", 768, "float32"), ("gs", 1024, "float32"),
+    ("blo pcb bmo ro1 ro3 lr1 lr3 zz", 16, "uint16"), ("r1 r3", 2, "uint16"), ("boff", 48, "uint16"), ("bpo", 64, "uint16"),
+    ("pco mo lam no rhoo l1", 128, "uint16"), ("nbo po", 384, "uint16"),
+    ("pc ub qb id16 kk kt", 16, "float32"), ("r4 r5", C, "float32"), ("g40", 320, "float32"), ("bp db", 48, "float32"),
+    ("xi", 160, "float32"), ("eall", 144, "float32"), ("gm gf idf ones va va2 w1s wm wl dn ta tb tc te", 128, "float32"),
+    ("ua pcf gt pz mt lt inc nn rho rn cmf", 128, "float32"), ("nbf pa da", 384, "float32"),
+    ("jm m16 m0 bs gbb bmask xcb mb xm xxb sb", 256, "float32"), ("pg", 768, "float32"), ("gs", 1024, "float32"),
     ("rt t1 t2 xx sx", EXT, "float32"), ("p1 p2 p3 yy", V, "float32"), ("sp", V + 8, "float32"))
-PSUM = {"ps": 2048, "a0": 512, "a1": 512, "a2": 512, "a3": 512}
+PSUM = {"gw": 1024, "v0": 512, "v1": 512, "a0": 512, "a1": 512, "a2": 512, "a3": 512}
 for _n in PSUM:
     SCRATCH[_n] = ("psum", [128, PSUM[_n]], "float32")
-EXCH = {"0": ("bli", "gl", 0, 2), "1": ("t1b", "t1", GH, C), "X": ("xb", "xe", GH, C), "2": ("m1b", "m1", GH, C),
-        "3": ("t2b", "t2", GH, C), "4": ("xxb", "xx", GH, C), "6": ("nxb", "nx", GH, C), "5": ("sb", "sx", GH, C)}
-ORDER = ["0", "1", "X", "2", "3", "4", "6", "5"]
-DMAS = ["bl", "gl", "nb", "w0", "w1", "w2", "x", "wb", "lo", "cm", "y0", "y1", "y2", "y3"]
+EXCH = {"X": ("xb", "xe", GH, C), "1": ("ro1", "lr1", 0, 2), "2": ("m1b", "m1", GH, C), "3": ("ro3", "lr3", 0, 2),
+        "4": ("xxb", "xx", GH, C), "6": ("nxb", "nx", GH, C), "5": ("sb", "sx", GH, C)}
+ORDER = ["X", "1", "2", "3", "4", "6", "5"]
+DMAS = ["bl", "z1", "z3", "nb", "w0", "w1", "w2", "x", "wb", "lo", "cm"] + ["y%d" % i for i in range(8)]
 SEMAPHORES = (["v", "s", "t", "p", "loc", "rloc"] + ["d" + n for n in DMAS] + ["arr" + k for k in ORDER]
               + ["hop" + k for k in ORDER])
 
@@ -106,23 +106,18 @@ def rank_program(g, core, T, topo):
         out = []
         for regs, wr in ((reads, False), (writes, True)):
             for name, lo, hi in regs:
-                if name in PSUM:
-                    lo, hi = lo // 512 * 512, -(-hi // 512) * 512
+                ps = name in PSUM
                 for l, h, w, tok, qq in log.get(name, []):
-                    if l < hi and lo < h:
-                        if name in PSUM:
-                            if qq == queue and (queue == "t" or not (w or wr)):
-                                continue
+                    if ps and qq != queue:
+                        if l // 512 * 512 < -(-hi // 512) * 512 and lo // 512 * 512 < -(-h // 512) * 512:
                             out.append(tok)
-                        elif w or wr:
-                            out.append(tok)
+                    elif l < hi and lo < h and (w or wr) and not (ps and queue == "t"):
+                        out.append(tok)
         return out
 
     def note(queue, reads, writes, tok):
         for regs, wr in ((reads, False), (writes, True)):
             for name, lo, hi in regs:
-                if name in PSUM:
-                    lo, hi = lo // 512 * 512, -(-hi // 512) * 512
                 log.setdefault(name, []).append((lo, hi, wr, tok, queue))
 
     def ap(r):
@@ -175,9 +170,6 @@ def rank_program(g, core, T, topo):
 
     def sa(out, a, scale, bias):
         run("s", [a], [out], lambda: g.scalar.activation(ap(out), ap(a), IDENT, bias=float(bias), scale=float(scale)))
-
-    def fill(out, c):
-        run("v", [], [out], lambda: g.vector.memset(ap(out), c))
 
     def iota(out, pattern, base, ch):
         run("g", [], [out], lambda: g.iota(ap(out), pattern, base, ch, allow_small_or_imprecise_dtypes=True))
@@ -238,28 +230,25 @@ def rank_program(g, core, T, topo):
         totals["arr" + k] = n
         note("net", [], [(land, c0, c0 + w * N)], ("arr" + k, n))
 
-    def alias(copy, land, src):
-        copy((land, GH + C * rank, GH + C * rank + C), (src, C * rank, C * rank + C))
+    def alias(land, src):
+        sc((land, GH + C * rank, GH + C * rank + C), (src, C * rank, C * rank + C))
 
     base = rank * V
+    own = (2 * rank, 2 * rank + 2)
     dma("y", "bl", T.bli[:], T.bl[:], [], [("bli", 0, 16)])
     for d in range(D):
         dma("s" if d == 1 else "y", "w%d" % d, T.wa[:, 128 * d:128 * d + 128], T.w[:, V * d:V * d + V], [],
             [("wa", 128 * d, 128 * d + 128)])
     dma("s", "nb", T.nbi[:], T.nb[:], [], [("nbi", 0, 384)])
-    dma("y", "gl", T.gl[:, 2 * rank:2 * rank + 2], T.bl[:, 2 * rank:2 * rank + 2], [], [("gl", 2 * rank, 2 * rank + 2)])
     dma("y", "x", T.xe[:, 0:V], T.x[:], [], [("xe", 0, V)])
 
     iota(("pi", 0, 1), [[1, 1]], 0, 1)
     iota(("xi", 0, 160), [[1, 160]], 0, 0)
     iota(("rt", 0, 512), [[1, 512]], base, 0)
-    send("0")
-    iota(("qc", 0, 256), [[V, N], [0, C]], -base, 0)
     iota(("gm", 0, 128), [[16, 8], [0, 16]], 0, 0)
-    iota(("va", 0, 128), [[16, 128]], base, 1)
-    iota(("lo", 0, 128), [[1, 128]], 0, 0)
-    iota(("hl", 0, V), [[1, 16], [0, 128]], 16 * rank, 0)
-    iota(("hl", GH, NONE), [[16, N], [0, C]], 0, 0)
+    iota(("jm", 0, 256), [[0, 16], [1, 16]], 0, 0)
+    iota(("kk", 0, 16), [[-C, N], [0, 2]], 40 * rank + 1 - GH, 0)
+    iota(("hl", 0, 1024), [[1, 8], [0, 128]], 16 * rank, 0)
 
     def col(i):
         return ("pc", i, i + 1)
@@ -275,12 +264,13 @@ def rank_program(g, core, T, topo):
     ts(("s1", 0, 160), ("xi", 0, 160), col(1), A.is_equal, col(3), A.mult)
     cp(col(4), ("pi", 1, 2))
     tt(col(5), ("pi", 0, 1), ("pi", 1, 2), A.subtract)
+    run("v", [], [("zz", 0, 16)], lambda: g.vector.memset(T.zz[:], 0))
+    ts(("id16", 0, 16), ("xi", 0, 16), col(4), A.is_equal)
+    for k in ("1", "3"):
+        dma("y", "z" + k, T["lr" + k][:, own[0]:own[1]], T.zz[:, 0:2], [("zz", 0, 2)], [("lr" + k,) + own])
     for i in range(1, 4):
         sa(("rt", 512 * i, 512 * i + 512), ("rt", 0, 512), 1, 512 * i)
-    sc(("ps", 0, V), ("rt", 0, V))
-    sa(("lw", 0, V), ("rt", 0, V), 0, -1)
-    sa(("lo", GH, NONE), ("rt", 0, 256), 0, 0)
-    sa(a("ones"), ("rt", 0, 128), 0, 1)
+    sa(("rt", NONE, NONE + 8), ("rt", 0, 8), 0, -1)
     run("v", [("wa", 0, 384)], [("tr", 0, 384)], lambda: g.vector.transpose(T.tr[:], T.wa[:]))
     for d in range(D):
         grp = []
@@ -292,106 +282,119 @@ def rank_program(g, core, T, topo):
                             ("tr", 128 * d + 32 * b + 16 * gg, 128 * d + 32 * b + 16 * gg + 16), gg == 0, gg == 1))
         mm(grp)
     cp(("nbf", 0, 384), ("nbi", 0, 384))
-    nb = [a("nbf", d) for d in range(D)]
-    tt(a("dn"), nb[1], nb[0], A.subtract)
+    sc(("v0", 0, 384), ("nbf", 0, 384))
+    nb, nbp = [a("nbf", d) for d in range(D)], [a("v0", d) for d in range(D)]
     cp(("blo", 0, 16), ("bli", 0, 16))
-    cp(("gbb", 0, 256), ("ind", ("rt", 0, V), ("blo", 0, 16)))
+    ts(("bms", 0, 16), ("bli", 0, 16), 15, A.bitwise_and)
     ts(("bsh", 0, 16), ("bli", 0, 16), 4, A.arith_shift_right)
-    cp(("gbi", 0, 256), ("gbb", 0, 256))
+    cp(("bmo", 0, 16), ("bms", 0, 16))
     for d in range(D):
         ts(("boff", 16 * d, 16 * d + 16), ("bsh", 0, 16), 128 * d, A.add)
-    ts(("gbi", 0, 256), ("gbi", 0, 256), 15, A.bitwise_and)
     ts(col(6), col(5), 15, A.add)
-    ts(("bmask", 0, 256), ("gbi", 0, 256), col(4), A.is_equal)
+    sc(("bmask", 0, 256), ("ind", ("id16", 0, 16), ("bmo", 0, 16)))
+    sc(("gbb", 0, 256), ("ind", ("rt", 0, V), ("blo", 0, 16)))
+    sa(("g40", 0, 320), ("rt", 0, 320), 0, -1)
+    for q in range(N):
+        sc(("g40", 40 * q + 1, 40 * q + 33), ("gbb", C * q, C * q + C))
+    sa(("rt", GH, NONE), ("rt", 0, 256), 0, -1)
+    alias("rt", "gbb")
+    sc(("xb", 0, 256), ("ind", ("xe", 0, V), ("blo", 0, 16)))
+    send("X")
+    alias("xe", "xb")
+    sc(("gw", 0, 1024), ("rt", 1024, V))
     ts(("eall", 0, 143), ("xi", 0, 143), col(6), A.is_equal)
-    fill(("rt", NONE, NONE + 8), -1.0)
+    ts(a("gf"), a("gm"), col(5), A.is_equal)
+    tt(a("dn"), nb[1], nbp[0], A.subtract)
+    tt(a("v1", 3), nb[0], nbp[1], A.add)
     cp(a("w1s"), a("a0", 1))
-    tt(a("g1"), a("w1s"), a("a0", 0), A.is_gt)
+    tt(a("v1", 0), a("w1s"), a("a0", 0), A.is_gt)
     tt(a("wm"), a("w1s"), a("a0", 0), A.max)
-    tt(a("ta"), a("g1"), a("dn"), A.mult)
-    tt(a("g2"), a("a0", 2), a("wm"), A.is_gt)
-    tt(a("tb"), a("ta"), nb[0], A.add)
-    tt(a("tc"), nb[2], a("tb"), A.subtract)
-    tt(a("td"), a("g2"), a("tc"), A.mult)
-    tt(a("pa"), a("tb"), a("td"), A.add)
-    cp(a("po"), a("pa"))
-    arrive("0")
-    cp(("glo", 0, 16), ("gl", 0, 16))
-    tt(("rt", GH, NONE), ("ind", ("rt", 0, V), ("glo", 0, 16)), ("qc", 0, 256), A.add)
-    cp(("t1", 0, 1024), ("ind", ("rt", 0, NONE + 8), ("po", 0, 64)))
-    sc(("t1", 1024, V), ("ind", ("rt", 0, NONE + 8), ("po", 64, 128)))
-    cp(("t1b", 0, 256), ("ind", ("t1", 0, V), ("blo", 0, 16)))
-    alias(cp, "t1", "t1b")
-    send("1")
+    tt(a("ta"), a("dn"), a("v1", 0), A.mult)
+    tt(a("v1", 1), a("a0", 2), a("wm"), A.is_gt)
+    tt(a("tb"), a("ta"), nbp[0], A.add)
+    tt(a("tc"), nbp[2], a("tb"), A.subtract)
+    tt(a("v1", 2), a("tc"), a("v1", 1), A.mult)
+    tt(a("pa"), a("tb"), a("v1", 2), A.add)
 
     def border(d):
         tt(("pg", 256 * d, 256 * d + 256), ("ind", ("pa", 0, 384 if d else 128), ("boff", 16 * d, 16 * d + 16)),
            ("bmask", 0, 256), A.mult)
     border(0)
-    to_a("a1", 0, 16, "eall", "pg", 0)
-    sc(("xb", 0, 256), ("ind", ("xe", 0, V), ("blo", 0, 16)))
-    alias(sc, "xe", "xb")
-    send("X")
-    for n in (128, 256, 512, 1024):
-        sc(("lo", n, 2 * n), ("lo", 0, n))
+    mm([(("a1", 0, 256), a("gf"), ("pg", 0, 256), True, True)])
+    cp(a("po"), a("pa"))
+    ts(("m16", 0, 256), ("jm", 0, 256), col(4), A.is_equal)
+    ts(("m0", 0, 256), ("jm", 0, 256), 0, A.is_gt)
+    tt(("bs", 0, 256), ("m16", 0, 256), ("a1", 0, 256), A.mult)
+    run("v", [("m0", 0, 256), ("bs", 0, 256)], [("pg", 0, 256)],
+        lambda: g.vector.tensor_tensor_scan(T.pg[:, 0:256], T.m0[:], T.bs[:], 0.0, A.mult, A.add))
+
+    def name_slots(out, src):
+        tt(("kt", 0, 16), src, ("kk", 0, 16), A.add)
+        ts((out, 0, 16), ("kt", 0, 16), 40 * rank, A.max, 40 * rank + 33, A.min)
+    name_slots("ro1", ("pg", 15, 256, 16))
+    send("1")
+    iota(("hl", 1024, V), [[1, 8], [0, 128]], 16 * rank + 8, 0)
+    iota(("hl", GH, NONE), [[16, N], [0, C]], 0, 0)
+    iota(("va", 0, 128), [[16, 128]], base, 1)
+    iota(("lo", 0, 128), [[1, 128]], 0, 0)
+    cp(("t1", 0, 1024), ("ind", ("rt", 0, NONE + 8), ("po", 0, 64)))
+    sc(("t1", 1024, V), ("ind", ("rt", 0, NONE + 8), ("po", 64, 128)))
+    cp(("bpo", 0, 16), ("pg", 15, 256, 16))
+    cp(("bp", 0, 16), ("pg", 15, 256, 16))
+    sc(("x2", 0, V), ("xe", 0, V))
     tt(a("wl"), a("w1s"), a("a0", 0), A.min)
-    tt(a("te"), nb[0], nb[1], A.add)
-    tt(a("g1"), a("a0", 2), a("wl"), A.is_gt)
-    tt(a("ta"), a("te"), a("tb"), A.subtract)
-    tt(a("te"), a("te"), nb[2], A.add)
-    tt(a("tc"), nb[2], a("ta"), A.subtract)
-    tt(a("te"), a("te"), a("pa"), A.subtract)
-    tt(a("td"), a("g1"), a("tc"), A.mult)
-    tt(a("pa", 2), nb[2], a("td"), A.subtract)
-    tt(a("pa", 1), a("te"), a("pa", 2), A.subtract)
+    tt(a("ta"), a("v1", 3), a("tb"), A.subtract)
+    tt(a("v1", 0), a("a0", 2), a("wl"), A.is_gt)
+    tt(a("tc"), nbp[2], a("ta"), A.subtract)
+    tt(a("v1", 3), nb[2], a("v1", 3), A.add)
+    tt(a("te"), a("tc"), a("v1", 0), A.mult)
+    tt(a("v1", 3), a("v1", 3), a("pa"), A.subtract)
+    tt(a("pa", 2), nbp[2], a("te"), A.subtract)
+    tt(a("pa", 1), a("v1", 3), a("pa", 2), A.subtract)
     border(1)
     border(2)
     to_a("a2", 0, 32, "eall", "pg", 256)
     ts(col(7), col(4), 0, A.is_equal)
     ts(col(8), col(4), 1, A.is_equal)
     ts(("e1", 0, 143), ("xi", 0, 143), col(6), A.is_equal, col(7), A.mult)
-    cp(("bpo", 0, 16), ("a1", 0, 16))
-    cp(("bp", 0, 16), ("a1", 0, 16))
+    ts(("nbo", 0, 384), ("nbf", 0, 384), 0, A.add)
+
+    def resolve(land, tab):
+        sc((tab, GH, NONE), ("ind", ("g40", 0, 320), (land, 0, 16)))
+        sc((tab, GH + C * rank, GH + C * rank + C), ("ind", (tab, 0, V), ("blo",) + own))
     arrive("1")
+    resolve("lr1", "t1")
     tt(("m1b", 0, 256), ("ind", ("t1", 0, NONE), ("bpo", 0, 16)), ("gbb", 0, 256), A.is_equal)
-    alias(cp, "m1", "m1b")
     send("2")
 
     def mutual(out, tab, lst, width, a0, a1):
         sc(("gs", 0, 1024), ("ind", (tab, 0, width), (lst, 64, 128)))
         tt((out, 0, 1024), ("ind", (tab, 0, width), (lst, 0, 64)), ("rt", 0, 1024), A.is_equal)
         to_a(a0[0], a0[1], 64, "e1", out, 0)
-        tt((out, 1024, V), ("gs", 0, 1024), ("ps", 1024, V), A.is_equal)
+        tt((out, 1024, V), ("gs", 0, 1024), ("gw", 0, 1024), A.is_equal)
         to_a(a1[0], a1[1], 64, "e1", out, 1024)
     mutual("m1", "t1", "po", NONE, ("a3", 0), ("a3", 64))
-    sc(("x2", 0, V), ("xe", 0, V))
-    cp(("po", 128, 384), ("pa", 128, 384))
+    alias("m1", "m1b")
+    sa(a("da", 2), a("pa", 2), -1, NONE)
+    sa(("lo", GH, NONE), ("rt", 0, 256), 0, 0)
+    for n in (128, 256, 512, 1024):
+        sc(("lo", n, 2 * n), ("lo", 0, n))
     dma("y", "lo", T.hl[1::16, 0:NONE], T.lo[1::16, 0:NONE], [("lo", 0, NONE)], [("hl", 0, NONE)])
+    cp(("po", 256, 384), a("pa", 2))
     cp(("bpo", 16, 48), ("a2", 0, 32))
     cp(("bp", 16, 48), ("a2", 0, 32))
     cp(("bpo", 48, 64), ("blo", 0, 16))
-    for buf, src, n in (("db", "bp", 16), ("da", "pa", 128)):
-        tt((buf, 0, n), (src, n, 2 * n), (src, 0, n), A.subtract)
-        tt((buf, n, 2 * n), (src, 2 * n, 3 * n), (src, n, 2 * n), A.subtract)
-        ts((buf, 2 * n, 3 * n), (src, 2 * n, 3 * n), -1, A.mult, NONE, A.add)
-    ts(a("qa"), a("a3"), -1, A.mult, 1, A.add)
-    tt(a("da", 0), a("da", 0), a("qa"), A.mult)
+    cp(("po", 128, 256), a("pa", 1))
+    tt(("db", 0, 16), ("bp", 16, 32), ("bp", 0, 16), A.subtract)
+    tt(("db", 16, 32), ("bp", 32, 48), ("bp", 16, 32), A.subtract)
+    sa(("db", 32, 48), ("bp", 32, 48), -1, NONE)
+    tt(a("ta"), a("pa", 1), a("pa", 0), A.subtract)
+    tt(a("v1", 0), a("pa", 2), a("pa", 1), A.subtract)
+    ts(a("v1", 1), a("a3"), -1, A.mult, 1, A.add)
+    tt(a("v1", 2), a("ta"), a("v1", 1), A.mult)
     for c in range(16):
         dma("y", "wb", T.wb[c::16, :], T.w[:], [("m1", 0, V)], [])
     note("y", [], [("wb", 0, 6144)], ("dwb", totals["dwb"]))
-    ts(a("va"), a("va"), col(5), A.subtract)
-    ts(a("gn"), a("gm"), col(5), A.is_equal)
-    ts(col(9), col(7), 128, A.mult)
-    ts(a("va2"), a("va"), V - base, A.add)
-    tt(col(10), col(8), col(9), A.add)
-    sa(a("go"), a("gn"), -1, 0)
-    ts(("ehl", 0, 143), ("xi", 0, 143), col(6), A.is_equal, col(10), A.mult)
-    fill(("t2", NONE, NONE + 8), -1.0)
-    fill(("xe", NONE, EXT), 0.0)
-    fill(("nx", NONE, EXT), 0.0)
-    fill(("sx", NONE, NONE + 8), 0.0)
-    fill(("sp", 0, 8), 0.0)
-    fill(("hl", NONE, EXT), 0.0)
     arrive("2")
     fl = ("m1", 0, NONE)
     sc(("fb", 0, 1024), ("ind", fl, ("bpo", 0, 64)))
@@ -410,10 +413,8 @@ def rank_program(g, core, T, topo):
     flags(sc, "f1", 0, 0)
     to_a("a1", 0, 64, "e1", "f3", 0)
     flags(cp, "f3", 2, 1)
-    to_a("a1", 64, 64, "e1", "f3", 1024)
-    flags(sc, "f1", 0, 1)
     to_a("a3", 0, 64, "e1", "f1", 0)
-    flags(cp, "f2", 1, 0)
+    to_a("a1", 64, 64, "e1", "f3", 1024)
     ts(("qb", 0, 16), ps16(3), -1, A.mult, 1, A.add)
     tt(ub, ps16(2), b16("db", 2), A.mult)
     tt(ub, ub, b16("db", 1), A.add)
@@ -422,53 +423,75 @@ def rank_program(g, core, T, topo):
     tt(ub, ub, ps16(0), A.mult)
     tt(ub, ub, ("qb", 0, 16), A.mult)
     tt(ub, ub, b16("bp", 0), A.add)
-    cp(("pcb", 0, 16), ub)
-    sc(("t2b", 0, 256), ("ind", ("rt", 0, NONE + 8), ("pcb", 0, 16)))
-    alias(sc, "t2", "t2b")
+    name_slots("ro3", ub)
     send("3")
-    run("g", [a("go")], [a("nt")], lambda: g.affine_select(T.nt[:], T.go[:], [[-1, 128]], A.is_ge, 0.0, 0, 1))
+    cp(("pcb", 0, 16), ub)
+    flags(sc, "f2", 1, 0)
+    flags(sc, "f2", 1, 1)
+    flags(sc, "f1", 0, 1)
     to_a("a2", 0, 64, "e1", "f2", 0)
-    to_a("a3", 64, 64, "e1", "f1", 1024)
-    flags(cp, "f2", 1, 1)
     to_a("a2", 64, 64, "e1", "f2", 1024)
+    to_a("a3", 64, 64, "e1", "f1", 1024)
     tt(ua, a("a1"), a("da", 2), A.mult)
-    tt(ua, ua, a("da", 1), A.add)
-    tt(ua, ua, a("qa"), A.mult)
-    tt(ua, ua, a("a2"), A.mult)
-    tt(ua, ua, a("da", 0), A.add)
-    tt(ua, ua, a("a3"), A.mult)
-    tt(a("pcf"), ua, a("pa"), A.add)
-    cp(a("pco"), a("pcf"))
-    full = ("rt", 0, NONE + 8)
-    cp(("t2", 0, 1024), ("ind", full, ("pco", 0, 64)))
-    sc(("t2", 1024, V), ("ind", full, ("pco", 64, 128)))
+    tt(ua, ua, a("v1", 0), A.add)
+    tt(ua, ua, a("v1", 1), A.mult)
+    sa(("xe", NONE, EXT), ("rt", 0, 16), 0, 0)
     arrive("X")
     sc(("xcb", 0, 256), ("ind", ("xe", 0, EXT), ("pcb", 0, 16)))
     sc(("a1", 0, 256), ("xcb", 0, 256))
     sc(("a1", 256, 512), ("xb", 0, 256))
-    ts(a("pz"), a("pcf"), -NONE, A.add)
-    cp(("hl", GH + C * rank, GH + C * rank + C), ("ind", ("hl", 0, V), ("blo", 2 * rank, 2 * rank + 2)))
+    sa(("t2", NONE, NONE + 8), ("rt", 0, 8), 0, -1)
+    ts(a("va"), a("va"), col(5), A.subtract)
+    ts(a("gn"), a("gm"), col(5), A.is_equal)
+    ts(col(9), col(7), 128, A.mult)
+    ts(a("va2"), a("va"), V - base, A.add)
+    tt(col(10), col(8), col(9), A.add)
+    ts(a("go"), a("gn"), -1, A.mult)
+    run("g", [a("go")], [a("nt")], lambda: g.affine_select(T.nt[:], T.go[:], [[-1, 128]], A.is_ge, 0.0, 0, 1))
+    ts(("ehl", 0, 143), ("xi", 0, 143), col(6), A.is_equal, col(10), A.mult)
+    ts(a("idf"), ("xi", 16, 144), col(1), A.is_equal)
+    tt(ua, ua, a("a2"), A.mult)
+    tt(ua, ua, a("v1", 2), A.add)
+    tt(a("v1", 3), ua, a("a3"), A.mult)
+    tt(a("pcf"), a("pa"), a("v1", 3), A.add)
+    cp(a("pco"), a("pcf"))
+    full = ("rt", 0, NONE + 8)
+    cp(("t2", 0, 1024), ("ind", full, ("pco", 0, 64)))
+    sc(("t2", 1024, V), ("ind", full, ("pco", 64, 128)))
     arrive("3")
+    resolve("lr3", "t2")
     tt(("mb", 0, 256), ("ind", ("t2", 0, NONE + 8), ("pcb", 0, 16)), ("gbb", 0, 256), A.is_equal)
     tt(("xm", 0, 256), ("mb", 0, 256), ("a1", 0, 256), A.mult)
     tt(("xxb", 0, 256), ("xm", 0, 256), ("a1", 256, 512), A.add)
     send("4")
     mutual("mm", "t2", "pco", NONE + 8, ("a0", 0), ("a2", 0))
-    alias(sc, "xx", "xxb")
+    sa(a("pz"), a("pcf"), 1, -NONE)
+    sa(("hl", NONE, EXT), ("rt", 0, 16), 0, 0)
+    sc(("hl", GH + C * rank, GH + C * rank + C), ("ind", ("hl", 0, V), ("blo",) + own))
+    alias("xx", "xxb")
     sc(("hg", 0, V), ("ind", ("hl", 0, EXT), ("pco", 0, 128)))
     to_a("a3", 0, 128, "ehl", "hg")
+    sa(a("ones"), ("rt", 0, 128), 0, 1)
     for h, ma in ((0, ("a0", 0, 64)), (1, ("a2", 0, 64))):
         c0, c1 = 64 * h, 64 * h + 64
         tt(("mt", c0, c1), ("pz", c0, c1), ma, A.mult)
         ts(("mo", c0, c1), ("mt", c0, c1), NONE, A.add)
         tt(("xx", 1024 * h, 1024 * h + 1024), ("ind", ("xe", 0, EXT), ("mo", c0, c1)), ("x2", 1024 * h, 1024 * h + 1024), A.add)
+
+    def weights(bank, d, lo, n):
+        sc((bank, 0, n), ("wb", V * d + lo, V * d + lo + n))
+    weights("gw", 2, 0, 1024)
+    weights("v0", 2, 1024, 512)
     tt(a("gt"), a("a3"), a("va"), A.is_gt)
     tt(("rep", 0, 64), ("gt", 0, 64), ("a0", 0, 64), A.is_ge)
     tt(("rep", 64, 128), ("gt", 64, 128), ("a2", 0, 64), A.is_ge)
+    weights("a0", 2, 1536, 512)
+    weights("a2", 1, 1024, 512)
     mm([(a("a1"), a("gn"), a("rep"), True, True)])
     mm([(a("a3"), a("nt"), a("rep"), True, True)])
-    ts(("nbo", 0, 384), ("nbf", 0, 384), 0, A.add)
-    ts(a("nr"), a("rep"), -1, A.mult, 1, A.add)
+    ts(a("v1", 1), a("rep"), -1, A.mult, 1, A.add)
+    tt(a("lt"), a("pz"), a("v1", 1), A.mult)
+    ts(a("lam"), a("lt"), NONE, A.add)
     run("v", [a("ones"), a("a1")], [a("inc")],
         lambda: g.vector.tensor_tensor_scan(T.inc[:], T.ones[:], T.a1[:, 0:128], 0.0, A.mult, A.add))
     tt(a("nn"), a("inc"), a("a3"), A.add)
@@ -478,39 +501,47 @@ def rank_program(g, core, T, topo):
         tt((buf, 1024 * h, 1024 * h + 1024), ("ind", ("xx", 0, NONE), ("nbo", 128 * d + 64 * h, 128 * d + 64 * h + 64)),
            ("wb", V * d + 1024 * h, V * d + 1024 * h + 1024), A.mult)
 
-    def half(buf, h):
-        return (buf, 1024 * h, 1024 * h + 1024)
-    for i in range(4):
-        sc(("a%d" % i, 0, 512), ("wb", 2 * V + 512 * i, 2 * V + 512 * i + 512))
-    for h in range(2):
-        sc(half("p3", h), ("ind", ("xx", 0, NONE), ("nbo", 256 + 64 * h, 320 + 64 * h)))
-        prod("p1", 0, h)
-        sc(half("ps", h), half("p1", h))
+    def gather(buf, d, h):
+        sc((buf, 1024 * h, 1024 * h + 1024), ("ind", ("xx", 0, NONE), ("nbo", 128 * d + 64 * h, 128 * d + 64 * h + 64)))
+    gather("p3", 2, 1)
+    weights("a3", 1, 1536, 512)
+    gather("p2", 1, 1)
+    gather("p3", 2, 0)
+    prod("p1", 0, 0)
+    prod("p1", 0, 1)
     cp(a("no"), a("nn"))
-    tt(a("lt"), a("pz"), a("nr"), A.mult)
     tt(a("rho"), a("va2"), a("nn"), A.subtract)
-    ts(a("lam"), a("lt"), NONE, A.add)
-    tt(a("rho"), a("rho"), a("nr"), A.mult)
-    ts(a("rn"), a("nn"), base, A.add)
-    tt(a("rho"), a("rho"), a("nn"), A.add)
-    tt(a("rn"), a("rn"), a("rep"), A.mult)
+    sa(a("rn"), a("nn"), 1, base)
+    tt(a("v1", 0), a("rho"), a("v1", 1), A.mult)
+    tt(a("rho"), a("nn"), a("v1", 0), A.add)
     cp(a("rhoo"), a("rho"))
+    sa(("nx", NONE, EXT), ("rt", 0, 16), 0, 0)
     sc(("nx", 0, V), ("ind", ("hl", 0, V), ("no", 0, 128)))
     sc(("nxb", 0, 256), ("ind", ("nx", 0, V), ("blo", 0, 16)))
-    alias(sc, "nx", "nxb")
     send("6")
-    for h in range(2):
-        prod("p2", 1, h)
-        tt(half("ps", h), half("p2", h), half("ps", h), A.add)
-    for h in range(2):
-        for i in (2 * h, 2 * h + 1):
-            c = (512 * i, 512 * i + 512)
-            tt(("p2",) + c, ("p3",) + c, ("a%d" % i, 0, 512), A.mult)
-        tt(half("sx", h), half("p2", h), half("ps", h), A.add)
-        sc(half("p3", h), half("sx", h))
-    cp(("sb", 0, 256), ("ind", ("sx", 0, V), ("blo", 0, 16)))
-    alias(cp, "sx", "sb")
+    alias("nx", "nxb")
+    sa(("lw", 0, V), ("rt", 0, V), 0, -1)
+    last = (1536, V)
+    tt(("p3",) + last, ("p3",) + last, ("a0", 0, 512), A.mult)
+    tt(("p2",) + last, ("p2",) + last, ("a3", 0, 512), A.mult)
+    mm([(("v1", 0, 512), a("idf"), (p,) + last, p == "p1", p == "p3") for p in ("p1", "p2", "p3")])
+    prod("p2", 1, 0)
+    for lo, n, bank, w1 in ((0, 1024, "gw", None), (1024, 512, "v0", "a2")):
+        acc = (bank, 0, n)
+        tt(acc, ("p3", lo, lo + n), acc, A.mult)
+        if w1:
+            tt(("p2", lo, lo + n), ("p2", lo, lo + n), (w1, 0, n), A.mult)
+        tt(acc, ("p2", lo, lo + n), acc, A.add)
+        tt(("sx", lo, lo + n), ("p1", lo, lo + n), acc, A.add)
+    sc(("sx",) + last, ("v1", 0, 512))
+    sc(("sb", 0, 256), ("ind", ("sx", 0, V), ("blo", 0, 16)))
     send("5")
+    alias("sx", "sb")
+    sc(("p3", 0, 1024), ("sx", 0, 1024))
+    sc(("gw", 0, 1024), ("sx", 1024, V))
+    sa(("sx", NONE, NONE + 8), ("rt", 0, 8), 0, 0)
+    sa(("sp", 0, 8), ("rt", 0, 8), 0, 0)
+    tt(a("cmf"), a("rn"), a("rep"), A.mult)
     run("v", [("hl", 0, V)], [("ind", ("lw", 0, 2 * V), ("rhoo", 0, 128))],
         lambda: g.vector.tensor_copy(ap(("ind", ("lw", 0, 2 * V), ("rhoo", 0, 128))), T.hl[:, 0:V]))
     to_a("a3", 0, 128, "ehl", "lw")
@@ -518,12 +549,14 @@ def rank_program(g, core, T, topo):
     sc(("cg", 0, V), ("ind", ("nx", 0, EXT), ("lam", 0, 128)))
     to_a("a1", 0, 128, "ehl", "cg")
     arrive("5")
-    tt(("sp", 8, V + 8), ("ind", ("sx", 0, NONE + 8), ("mo", 0, 128)), ("p3", 0, V), A.add)
+    sc(("p1", 1024, V), ("ind", ("sx", 0, NONE + 8), ("mo", 64, 128)))
+    tt(("sp", 8, 1032), ("ind", ("sx", 0, NONE + 8), ("mo", 0, 64)), ("p3", 0, 1024), A.add)
+    tt(("sp", 1032, V + 8), ("p1", 1024, V), ("gw", 0, 1024), A.add)
     ts(a("l1"), a("a3"), 8 - base, A.add, 0, A.max)
-    for i, eng in ((0, cp), (2, sc), (1, cp), (3, sc)):
-        eng(("yy", 512 * i, 512 * i + 512), ("ind", ("sp", 0, V + 8), ("l1", 32 * i, 32 * i + 32)))
-    for i in (0, 2, 1, 3):
-        dma("y", "y%d" % i, T.y[:, 512 * i:512 * i + 512], T.yy[:, 512 * i:512 * i + 512], [("yy", 512 * i, 512 * i + 512)], [])
-    tt(a("cmf"), a("rn"), a("a1"), A.add)
+    for i in range(8):
+        (sc if i % 2 else cp)(("yy", 256 * i, 256 * i + 256), ("ind", ("sp", 0, V + 8), ("l1", 16 * i, 16 * i + 16)))
+    for i in range(8):
+        dma("y", "y%d" % i, T.y[:, 256 * i:256 * i + 256], T.yy[:, 256 * i:256 * i + 256], [("yy", 256 * i, 256 * i + 256)], [])
+    tt(a("cmf"), a("cmf"), a("a1"), A.add)
     dma("y", "cm", T.cm[:], T.cmf[:], [a("cmf")], [])
     need("g", [("loc", sent[0])] + [(s, count[s]) for s in ("v", "s", "t", "p")] + sorted(totals.items()))

from concourse.mybir import AluOpType, ActivationFunctionType
from concourse.bass import DstId, RemoteDMATransfer

N, V, C, D = 8, 2048, 32, 3
GH, NONE = V, V + N * C
EXT = NONE + 16


def buffers(*groups):
    out = {}
    for names, width, dtype in groups:
        for n in names.split():
            out[n] = ("sbuf", [128, width], dtype)
    return out


SCRATCH = buffers(
    ("bli bsh bms", 16, "int32"), ("nbi", 384, "int32"), ("pi", 8, "int32"),
    ("wa tr", 384, "bfloat16"), ("wb", 6144, "bfloat16"), ("s0 s1", 160, "bfloat16"), ("e1 ehl", 144, "bfloat16"),
    ("gn go nt rep", 128, "bfloat16"), ("xe hl m1 nx", EXT, "bfloat16"), ("lo", NONE, "bfloat16"),
    ("xb m1b nxb", 256, "bfloat16"), ("fb", 1024, "bfloat16"), ("f1 f2 f3 mm hg cg x2", V, "bfloat16"),
    ("lw", 2 * V, "bfloat16"), ("rX r2 r6", C, "bfloat16"),
    ("blo pcb bmo ro1 ro3 lr1 lr3 zz", 16, "uint16"), ("r1 r3", 2, "uint16"), ("boff", 48, "uint16"), ("bpo", 64, "uint16"),
    ("pco mo lam no rhoo l1", 128, "uint16"), ("nbo po", 384, "uint16"),
    ("pc ub qb id16 kk kt", 16, "float32"), ("r4 r5", C, "float32"), ("g40", 320, "float32"), ("bp db", 48, "float32"),
    ("xi", 160, "float32"), ("eall", 144, "float32"), ("gm gf idf ones va va2 w1s wm wl dn ta tb tc te", 128, "float32"),
    ("ua pcf gt pz mt lt inc nn rho rn cmf", 128, "float32"), ("nbf pa da", 384, "float32"),
    ("jm m16 m0 bs gbb bmask xcb mb xm xxb sb", 256, "float32"), ("pg", 768, "float32"), ("gs", 1024, "float32"),
    ("rt t1 t2 xx sx", EXT, "float32"), ("p1 p2 p3 yy", V, "float32"), ("sp", V + 8, "float32"))
PSUM = {"gw": 1024, "v0": 512, "v1": 512, "a0": 512, "a1": 512, "a2": 512, "a3": 512}
for _n in PSUM:
    SCRATCH[_n] = ("psum", [128, PSUM[_n]], "float32")
EXCH = {"X": ("xb", "xe", GH, C), "1": ("ro1", "lr1", 0, 2), "2": ("m1b", "m1", GH, C), "3": ("ro3", "lr3", 0, 2),
        "4": ("xxb", "xx", GH, C), "6": ("nxb", "nx", GH, C), "5": ("sb", "sx", GH, C)}
ORDER = ["X", "1", "2", "3", "4", "6", "5"]
DMAS = ["bl", "z1", "z3", "nb", "w0", "w1", "w2", "x", "wb", "lo", "cm"] + ["y%d" % i for i in range(8)]
SEMAPHORES = (["v", "s", "t", "p", "loc", "rloc"] + ["d" + n for n in DMAS] + ["arr" + k for k in ORDER]
              + ["hop" + k for k in ORDER])


def pick(engines, i, n):
    m = 0
    for e in engines[i * n:(i + 1) * n]:
        m |= 1 << e
    return m


def plan(src, T, topo):
    near, far = [], []
    for d in T.cores:
        if d != src:
            (near if topo.may_write(src, d) else far).append(d)
    hops = [c for c in topo.cores_of(src) if c != src and all(topo.may_write(c, d) for d in far)]
    straight = [(d, pick(topo.engines(src, d), i, 2)) for i, d in enumerate(near)]
    over = []
    for i, d in enumerate(far):
        h = hops[i]
        over.append((h, pick(topo.engines(src, h), i, 4), d, topo.mask(h, d)))
    return straight, over


def bits(m):
    return bin(m).count("1")


def hop_program(g, core, T, topo):
    for src in topo.cores_of(core):
        if T.rank_of(src) is None:
            continue
        r = T.rank_of(src)
        for h, m_in, d, m_out in plan(src, T, topo)[1]:
            if h != core:
                continue
            rid, pid = topo.addr(d, core)
            for k in ORDER:
                _, land, c0, w = EXCH[k]
                g.wait_ge(T.sem["hop" + k], bits(m_in))
                g.remote_dma(T[land][:, c0 + w * r:c0 + w * r + w], T["r" + k][:], T.sem["arr" + k], T.sem.rloc,
                             pid, rid, m_out)
            g.wait_ge(T.sem.rloc, bits(m_out) * len(ORDER))


def rank_program(g, core, T, topo):
    rank = T.rank_of(core)
    if rank is None:
        hop_program(g, core, T, topo)
        return
    A = AluOpType
    COPY, IDENT = ActivationFunctionType.Copy, ActivationFunctionType.Identity
    q_of = {"v": g.vector, "s": g.scalar, "t": g.tensor, "g": g, "y": g.sync}
    count = {"v": 0, "s": 0, "t": 0, "p": 0}
    waited = {"v": {}, "s": {}, "t": {}, "g": {}, "y": {}}
    log = {}
    totals = {}

    def need(queue, tokens):
        best = {}
        for s, n in tokens:
            best[s] = max(n, best.get(s, 0))
        for s in sorted(best):
            if waited[queue].get(s, 0) < best[s]:
                q_of[queue].wait_ge(T.sem[s], best[s])
                waited[queue][s] = best[s]

    def deps(queue, reads, writes):
        out = []
        for regs, wr in ((reads, False), (writes, True)):
            for name, lo, hi in regs:
                ps = name in PSUM
                for l, h, w, tok, qq in log.get(name, []):
                    if ps and qq != queue:
                        if l // 512 * 512 < -(-hi // 512) * 512 and lo // 512 * 512 < -(-h // 512) * 512:
                            out.append(tok)
                    elif l < hi and lo < h and (w or wr) and not (ps and queue == "t"):
                        out.append(tok)
        return out

    def note(queue, reads, writes, tok):
        for regs, wr in ((reads, False), (writes, True)):
            for name, lo, hi in regs:
                log.setdefault(name, []).append((lo, hi, wr, tok, queue))

    def ap(r):
        if r[0] == "ind":
            return ap(r[1]).indirect(ap(r[2]))
        name, lo, hi = r[0], r[1], r[2]
        return T[name][:, lo:hi] if len(r) == 3 else T[name][:, lo:hi:r[3]]

    def regs(rs):
        out = []
        for r in rs:
            if isinstance(r, tuple):
                if r[0] == "ind":
                    out += regs([r[1], r[2]])
                else:
                    out.append((r[0], r[1], r[2]))
        return out

    def val(x):
        return ap(x) if isinstance(x, tuple) else x

    def run(queue, reads, outs, emit):
        rd, wr = regs(reads), []
        for o in outs:
            if o[0] == "ind":
                wr += regs([o[1]])
                rd += regs([o[2]])
            else:
                wr += regs([o])
        need(queue, deps(queue, rd, wr))
        s = "p" if queue == "g" else queue
        count[s] += 1
        emit().then_inc(T.sem[s], 1)
        note(queue, rd, wr, (s, count[s]))

    def tt(out, a, b, op):
        run("v", [a, b], [out], lambda: g.vector.tensor_tensor(ap(out), ap(a), ap(b), op))

    def ts(out, a, s1, op0, s2=None, op1=None):
        if op1 is None:
            run("v", [a, s1], [out], lambda: g.vector.tensor_scalar(ap(out), ap(a), val(s1), None, op0))
        else:
            run("v", [a, s1, s2], [out], lambda: g.vector.tensor_scalar(ap(out), ap(a), val(s1), val(s2), op0, op1))

    def cp(out, a):
        run("v", [a], [out], lambda: g.vector.tensor_copy(ap(out), ap(a)))

    def sc(out, a):
        run("s", [a], [out], lambda: g.scalar.activation(ap(out), ap(a), COPY))

    def sa(out, a, scale, bias):
        run("s", [a], [out], lambda: g.scalar.activation(ap(out), ap(a), IDENT, bias=float(bias), scale=float(scale)))

    def iota(out, pattern, base, ch):
        run("g", [], [out], lambda: g.iota(ap(out), pattern, base, ch, allow_small_or_imprecise_dtypes=True))

    def mm(group):
        rd = regs([m[1] for m in group] + [m[2] for m in group])
        wr = regs([m[0] for m in group])
        need("t", deps("t", rd, wr))
        ins = None
        for o, l, r, st, sp in group:
            ins = g.tensor.matmul(ap(o), ap(l), ap(r), st, sp)
        count["t"] += 1
        ins.then_inc(T.sem.t, 1)
        note("t", list(dict.fromkeys(rd)), list(dict.fromkeys(wr)), ("t", count["t"]))

    def to_a(ps, c0, n, lhs, src, base=0):
        mm([((ps, c0, c0 + n), (lhs, 15 - k, 143 - k), (src, base + k, base + 16 * n, 16), k == 0, k == 15)
            for k in range(16)])

    def dma(queue, sem, out, in_, reads, writes):
        need(queue, deps(queue, reads, writes))
        q_of[queue].dma_start(out, in_).then_inc(T.sem["d" + sem], 16)
        totals["d" + sem] = totals.get("d" + sem, 0) + 16
        note(queue, reads, writes, ("d" + sem, totals["d" + sem]))

    straight, over = plan(core, T, topo)
    sent = [0]

    def send(k):
        src, land, c0, w = EXCH[k]
        need("g", deps("g", [(src, 0, w * N)], []))

        def block(d):
            q = T.rank_of(d)
            return T[src][:, w * q:w * q + w]
        calls = []
        for h, m_in, d, _ in over:
            rid, pid = topo.addr(h, core)
            calls.append(RemoteDMATransfer(dst_ids=[DstId(rid=rid, pnc=pid)], dma_engine_mask=m_in, remote_sem=T.sem["hop" + k],
                                           src=block(d), dst=T["r" + k][:]))
            sent[0] += bits(m_in)
        g.remote_dma_fused(calls, local_sem=T.sem.loc)
        calls = []
        for d, m in straight:
            rid, pid = topo.addr(d, core)
            calls.append(RemoteDMATransfer(dst_ids=[DstId(rid=rid, pnc=pid)], dma_engine_mask=m, remote_sem=T.sem["arr" + k],
                                           src=block(d), dst=T[land][:, c0 + w * rank:c0 + w * rank + w]))
            sent[0] += bits(m)
        g.remote_dma_fused(calls, local_sem=T.sem.loc)

    def arrive(k):
        n = 0
        for c in T.cores:
            if c != core:
                near, far = plan(c, T, topo)
                n += sum(bits(m) for d, m in near if d == core) + sum(bits(m) for _, _, d, m in far if d == core)
        _, land, c0, w = EXCH[k]
        totals["arr" + k] = n
        note("net", [], [(land, c0, c0 + w * N)], ("arr" + k, n))

    def alias(land, src):
        sc((land, GH + C * rank, GH + C * rank + C), (src, C * rank, C * rank + C))

    base = rank * V
    own = (2 * rank, 2 * rank + 2)
    dma("y", "bl", T.bli[:], T.bl[:], [], [("bli", 0, 16)])
    for d in range(D):
        dma("s" if d == 1 else "y", "w%d" % d, T.wa[:, 128 * d:128 * d + 128], T.w[:, V * d:V * d + V], [],
            [("wa", 128 * d, 128 * d + 128)])
    dma("s", "nb", T.nbi[:], T.nb[:], [], [("nbi", 0, 384)])
    dma("y", "x", T.xe[:, 0:V], T.x[:], [], [("xe", 0, V)])

    iota(("pi", 0, 1), [[1, 1]], 0, 1)
    iota(("xi", 0, 160), [[1, 160]], 0, 0)
    iota(("rt", 0, 512), [[1, 512]], base, 0)
    iota(("gm", 0, 128), [[16, 8], [0, 16]], 0, 0)
    iota(("jm", 0, 256), [[0, 16], [1, 16]], 0, 0)
    iota(("kk", 0, 16), [[-C, N], [0, 2]], 40 * rank + 1 - GH, 0)
    iota(("hl", 0, 1024), [[1, 8], [0, 128]], 16 * rank, 0)

    def col(i):
        return ("pc", i, i + 1)

    def a(name, i=0):
        return (name, 128 * i, 128 * i + 128)
    ts(("pi", 2, 3), ("pi", 0, 1), 4, A.arith_shift_right, 1, A.bitwise_and)
    ts(("pi", 1, 2), ("pi", 0, 1), 15, A.bitwise_and)
    ts(col(1), ("pi", 0, 1), 16, A.add)
    cp(col(3), ("pi", 2, 3))
    ts(col(2), ("pi", 2, 3), -1, A.mult, 1, A.add)
    ts(("s0", 0, 160), ("xi", 0, 160), col(1), A.is_equal, col(2), A.mult)
    ts(("s1", 0, 160), ("xi", 0, 160), col(1), A.is_equal, col(3), A.mult)
    cp(col(4), ("pi", 1, 2))
    tt(col(5), ("pi", 0, 1), ("pi", 1, 2), A.subtract)
    run("v", [], [("zz", 0, 16)], lambda: g.vector.memset(T.zz[:], 0))
    ts(("id16", 0, 16), ("xi", 0, 16), col(4), A.is_equal)
    for k in ("1", "3"):
        dma("y", "z" + k, T["lr" + k][:, own[0]:own[1]], T.zz[:, 0:2], [("zz", 0, 2)], [("lr" + k,) + own])
    for i in range(1, 4):
        sa(("rt", 512 * i, 512 * i + 512), ("rt", 0, 512), 1, 512 * i)
    sa(("rt", NONE, NONE + 8), ("rt", 0, 8), 0, -1)
    run("v", [("wa", 0, 384)], [("tr", 0, 384)], lambda: g.vector.transpose(T.tr[:], T.wa[:]))
    for d in range(D):
        grp = []
        for i in range(8):
            b, h = i // 2, i % 2
            for gg in range(2):
                st = 16 - 16 * (gg - h)
                grp.append((("a0", 128 * d + i, 128 * d + 128, 8), ("s%d" % h, st, st + 128),
                            ("tr", 128 * d + 32 * b + 16 * gg, 128 * d + 32 * b + 16 * gg + 16), gg == 0, gg == 1))
        mm(grp)
    cp(("nbf", 0, 384), ("nbi", 0, 384))
    sc(("v0", 0, 384), ("nbf", 0, 384))
    nb, nbp = [a("nbf", d) for d in range(D)], [a("v0", d) for d in range(D)]
    cp(("blo", 0, 16), ("bli", 0, 16))
    ts(("bms", 0, 16), ("bli", 0, 16), 15, A.bitwise_and)
    ts(("bsh", 0, 16), ("bli", 0, 16), 4, A.arith_shift_right)
    cp(("bmo", 0, 16), ("bms", 0, 16))
    for d in range(D):
        ts(("boff", 16 * d, 16 * d + 16), ("bsh", 0, 16), 128 * d, A.add)
    ts(col(6), col(5), 15, A.add)
    sc(("bmask", 0, 256), ("ind", ("id16", 0, 16), ("bmo", 0, 16)))
    sc(("gbb", 0, 256), ("ind", ("rt", 0, V), ("blo", 0, 16)))
    sa(("g40", 0, 320), ("rt", 0, 320), 0, -1)
    for q in range(N):
        sc(("g40", 40 * q + 1, 40 * q + 33), ("gbb", C * q, C * q + C))
    sa(("rt", GH, NONE), ("rt", 0, 256), 0, -1)
    alias("rt", "gbb")
    sc(("xb", 0, 256), ("ind", ("xe", 0, V), ("blo", 0, 16)))
    send("X")
    alias("xe", "xb")
    sc(("gw", 0, 1024), ("rt", 1024, V))
    ts(("eall", 0, 143), ("xi", 0, 143), col(6), A.is_equal)
    ts(a("gf"), a("gm"), col(5), A.is_equal)
    tt(a("dn"), nb[1], nbp[0], A.subtract)
    tt(a("v1", 3), nb[0], nbp[1], A.add)
    cp(a("w1s"), a("a0", 1))
    tt(a("v1", 0), a("w1s"), a("a0", 0), A.is_gt)
    tt(a("wm"), a("w1s"), a("a0", 0), A.max)
    tt(a("ta"), a("dn"), a("v1", 0), A.mult)
    tt(a("v1", 1), a("a0", 2), a("wm"), A.is_gt)
    tt(a("tb"), a("ta"), nbp[0], A.add)
    tt(a("tc"), nbp[2], a("tb"), A.subtract)
    tt(a("v1", 2), a("tc"), a("v1", 1), A.mult)
    tt(a("pa"), a("tb"), a("v1", 2), A.add)

    def border(d):
        tt(("pg", 256 * d, 256 * d + 256), ("ind", ("pa", 0, 384 if d else 128), ("boff", 16 * d, 16 * d + 16)),
           ("bmask", 0, 256), A.mult)
    border(0)
    mm([(("a1", 0, 256), a("gf"), ("pg", 0, 256), True, True)])
    cp(a("po"), a("pa"))
    ts(("m16", 0, 256), ("jm", 0, 256), col(4), A.is_equal)
    ts(("m0", 0, 256), ("jm", 0, 256), 0, A.is_gt)
    tt(("bs", 0, 256), ("m16", 0, 256), ("a1", 0, 256), A.mult)
    run("v", [("m0", 0, 256), ("bs", 0, 256)], [("pg", 0, 256)],
        lambda: g.vector.tensor_tensor_scan(T.pg[:, 0:256], T.m0[:], T.bs[:], 0.0, A.mult, A.add))

    def name_slots(out, src):
        tt(("kt", 0, 16), src, ("kk", 0, 16), A.add)
        ts((out, 0, 16), ("kt", 0, 16), 40 * rank, A.max, 40 * rank + 33, A.min)
    name_slots("ro1", ("pg", 15, 256, 16))
    send("1")
    iota(("hl", 1024, V), [[1, 8], [0, 128]], 16 * rank + 8, 0)
    iota(("hl", GH, NONE), [[16, N], [0, C]], 0, 0)
    iota(("va", 0, 128), [[16, 128]], base, 1)
    iota(("lo", 0, 128), [[1, 128]], 0, 0)
    cp(("t1", 0, 1024), ("ind", ("rt", 0, NONE + 8), ("po", 0, 64)))
    sc(("t1", 1024, V), ("ind", ("rt", 0, NONE + 8), ("po", 64, 128)))
    cp(("bpo", 0, 16), ("pg", 15, 256, 16))
    cp(("bp", 0, 16), ("pg", 15, 256, 16))
    sc(("x2", 0, V), ("xe", 0, V))
    tt(a("wl"), a("w1s"), a("a0", 0), A.min)
    tt(a("ta"), a("v1", 3), a("tb"), A.subtract)
    tt(a("v1", 0), a("a0", 2), a("wl"), A.is_gt)
    tt(a("tc"), nbp[2], a("ta"), A.subtract)
    tt(a("v1", 3), nb[2], a("v1", 3), A.add)
    tt(a("te"), a("tc"), a("v1", 0), A.mult)
    tt(a("v1", 3), a("v1", 3), a("pa"), A.subtract)
    tt(a("pa", 2), nbp[2], a("te"), A.subtract)
    tt(a("pa", 1), a("v1", 3), a("pa", 2), A.subtract)
    border(1)
    border(2)
    to_a("a2", 0, 32, "eall", "pg", 256)
    ts(col(7), col(4), 0, A.is_equal)
    ts(col(8), col(4), 1, A.is_equal)
    ts(("e1", 0, 143), ("xi", 0, 143), col(6), A.is_equal, col(7), A.mult)
    ts(("nbo", 0, 384), ("nbf", 0, 384), 0, A.add)

    def resolve(land, tab):
        sc((tab, GH, NONE), ("ind", ("g40", 0, 320), (land, 0, 16)))
        sc((tab, GH + C * rank, GH + C * rank + C), ("ind", (tab, 0, V), ("blo",) + own))
    arrive("1")
    resolve("lr1", "t1")
    tt(("m1b", 0, 256), ("ind", ("t1", 0, NONE), ("bpo", 0, 16)), ("gbb", 0, 256), A.is_equal)
    send("2")

    def mutual(out, tab, lst, width, a0, a1):
        sc(("gs", 0, 1024), ("ind", (tab, 0, width), (lst, 64, 128)))
        tt((out, 0, 1024), ("ind", (tab, 0, width), (lst, 0, 64)), ("rt", 0, 1024), A.is_equal)
        to_a(a0[0], a0[1], 64, "e1", out, 0)
        tt((out, 1024, V), ("gs", 0, 1024), ("gw", 0, 1024), A.is_equal)
        to_a(a1[0], a1[1], 64, "e1", out, 1024)
    mutual("m1", "t1", "po", NONE, ("a3", 0), ("a3", 64))
    alias("m1", "m1b")
    sa(a("da", 2), a("pa", 2), -1, NONE)
    sa(("lo", GH, NONE), ("rt", 0, 256), 0, 0)
    for n in (128, 256, 512, 1024):
        sc(("lo", n, 2 * n), ("lo", 0, n))
    dma("y", "lo", T.hl[1::16, 0:NONE], T.lo[1::16, 0:NONE], [("lo", 0, NONE)], [("hl", 0, NONE)])
    cp(("po", 256, 384), a("pa", 2))
    cp(("bpo", 16, 48), ("a2", 0, 32))
    cp(("bp", 16, 48), ("a2", 0, 32))
    cp(("bpo", 48, 64), ("blo", 0, 16))
    cp(("po", 128, 256), a("pa", 1))
    tt(("db", 0, 16), ("bp", 16, 32), ("bp", 0, 16), A.subtract)
    tt(("db", 16, 32), ("bp", 32, 48), ("bp", 16, 32), A.subtract)
    sa(("db", 32, 48), ("bp", 32, 48), -1, NONE)
    tt(a("ta"), a("pa", 1), a("pa", 0), A.subtract)
    tt(a("v1", 0), a("pa", 2), a("pa", 1), A.subtract)
    ts(a("v1", 1), a("a3"), -1, A.mult, 1, A.add)
    tt(a("v1", 2), a("ta"), a("v1", 1), A.mult)
    for c in range(16):
        dma("y", "wb", T.wb[c::16, :], T.w[:], [("m1", 0, V)], [])
    note("y", [], [("wb", 0, 6144)], ("dwb", totals["dwb"]))
    arrive("2")
    fl = ("m1", 0, NONE)
    sc(("fb", 0, 1024), ("ind", fl, ("bpo", 0, 64)))
    to_a("a0", 0, 64, "e1", "fb")

    def flags(eng, f, d, h):
        eng((f, 1024 * h, 1024 * h + 1024), ("ind", fl, ("po", 128 * d + 64 * h, 128 * d + 64 * h + 64)))

    def ps16(i):
        return ("a0", 16 * i, 16 * i + 16)

    def b16(n, i):
        return (n, 16 * i, 16 * i + 16)
    ub, ua = ("ub", 0, 16), a("ua")
    flags(cp, "f3", 2, 0)
    flags(sc, "f1", 0, 0)
    to_a("a1", 0, 64, "e1", "f3", 0)
    flags(cp, "f3", 2, 1)
    to_a("a3", 0, 64, "e1", "f1", 0)
    to_a("a1", 64, 64, "e1", "f3", 1024)
    ts(("qb", 0, 16), ps16(3), -1, A.mult, 1, A.add)
    tt(ub, ps16(2), b16("db", 2), A.mult)
    tt(ub, ub, b16("db", 1), A.add)
    tt(ub, ub, ps16(1), A.mult)
    tt(ub, ub, b16("db", 0), A.add)
    tt(ub, ub, ps16(0), A.mult)
    tt(ub, ub, ("qb", 0, 16), A.mult)
    tt(ub, ub, b16("bp", 0), A.add)
    name_slots("ro3", ub)
    send("3")
    cp(("pcb", 0, 16), ub)
    flags(sc, "f2", 1, 0)
    flags(sc, "f2", 1, 1)
    flags(sc, "f1", 0, 1)
    to_a("a2", 0, 64, "e1", "f2", 0)
    to_a("a2", 64, 64, "e1", "f2", 1024)
    to_a("a3", 64, 64, "e1", "f1", 1024)
    tt(ua, a("a1"), a("da", 2), A.mult)
    tt(ua, ua, a("v1", 0), A.add)
    tt(ua, ua, a("v1", 1), A.mult)
    sa(("xe", NONE, EXT), ("rt", 0, 16), 0, 0)
    arrive("X")
    sc(("xcb", 0, 256), ("ind", ("xe", 0, EXT), ("pcb", 0, 16)))
    sc(("a1", 0, 256), ("xcb", 0, 256))
    sc(("a1", 256, 512), ("xb", 0, 256))
    sa(("t2", NONE, NONE + 8), ("rt", 0, 8), 0, -1)
    ts(a("va"), a("va"), col(5), A.subtract)
    ts(a("gn"), a("gm"), col(5), A.is_equal)
    ts(col(9), col(7), 128, A.mult)
    ts(a("va2"), a("va"), V - base, A.add)
    tt(col(10), col(8), col(9), A.add)
    ts(a("go"), a("gn"), -1, A.mult)
    run("g", [a("go")], [a("nt")], lambda: g.affine_select(T.nt[:], T.go[:], [[-1, 128]], A.is_ge, 0.0, 0, 1))
    ts(("ehl", 0, 143), ("xi", 0, 143), col(6), A.is_equal, col(10), A.mult)
    ts(a("idf"), ("xi", 16, 144), col(1), A.is_equal)
    tt(ua, ua, a("a2"), A.mult)
    tt(ua, ua, a("v1", 2), A.add)
    tt(a("v1", 3), ua, a("a3"), A.mult)
    tt(a("pcf"), a("pa"), a("v1", 3), A.add)
    cp(a("pco"), a("pcf"))
    full = ("rt", 0, NONE + 8)
    cp(("t2", 0, 1024), ("ind", full, ("pco", 0, 64)))
    sc(("t2", 1024, V), ("ind", full, ("pco", 64, 128)))
    arrive("3")
    resolve("lr3", "t2")
    tt(("mb", 0, 256), ("ind", ("t2", 0, NONE + 8), ("pcb", 0, 16)), ("gbb", 0, 256), A.is_equal)
    tt(("xm", 0, 256), ("mb", 0, 256), ("a1", 0, 256), A.mult)
    tt(("xxb", 0, 256), ("xm", 0, 256), ("a1", 256, 512), A.add)
    send("4")
    mutual("mm", "t2", "pco", NONE + 8, ("a0", 0), ("a2", 0))
    sa(a("pz"), a("pcf"), 1, -NONE)
    sa(("hl", NONE, EXT), ("rt", 0, 16), 0, 0)
    sc(("hl", GH + C * rank, GH + C * rank + C), ("ind", ("hl", 0, V), ("blo",) + own))
    alias("xx", "xxb")
    sc(("hg", 0, V), ("ind", ("hl", 0, EXT), ("pco", 0, 128)))
    to_a("a3", 0, 128, "ehl", "hg")
    sa(a("ones"), ("rt", 0, 128), 0, 1)
    for h, ma in ((0, ("a0", 0, 64)), (1, ("a2", 0, 64))):
        c0, c1 = 64 * h, 64 * h + 64
        tt(("mt", c0, c1), ("pz", c0, c1), ma, A.mult)
        ts(("mo", c0, c1), ("mt", c0, c1), NONE, A.add)
        tt(("xx", 1024 * h, 1024 * h + 1024), ("ind", ("xe", 0, EXT), ("mo", c0, c1)), ("x2", 1024 * h, 1024 * h + 1024), A.add)

    def weights(bank, d, lo, n):
        sc((bank, 0, n), ("wb", V * d + lo, V * d + lo + n))
    weights("gw", 2, 0, 1024)
    weights("v0", 2, 1024, 512)
    tt(a("gt"), a("a3"), a("va"), A.is_gt)
    tt(("rep", 0, 64), ("gt", 0, 64), ("a0", 0, 64), A.is_ge)
    tt(("rep", 64, 128), ("gt", 64, 128), ("a2", 0, 64), A.is_ge)
    weights("a0", 2, 1536, 512)
    weights("a2", 1, 1024, 512)
    mm([(a("a1"), a("gn"), a("rep"), True, True)])
    mm([(a("a3"), a("nt"), a("rep"), True, True)])
    ts(a("v1", 1), a("rep"), -1, A.mult, 1, A.add)
    tt(a("lt"), a("pz"), a("v1", 1), A.mult)
    ts(a("lam"), a("lt"), NONE, A.add)
    run("v", [a("ones"), a("a1")], [a("inc")],
        lambda: g.vector.tensor_tensor_scan(T.inc[:], T.ones[:], T.a1[:, 0:128], 0.0, A.mult, A.add))
    tt(a("nn"), a("inc"), a("a3"), A.add)
    arrive("4")

    def prod(buf, d, h):
        tt((buf, 1024 * h, 1024 * h + 1024), ("ind", ("xx", 0, NONE), ("nbo", 128 * d + 64 * h, 128 * d + 64 * h + 64)),
           ("wb", V * d + 1024 * h, V * d + 1024 * h + 1024), A.mult)

    def gather(buf, d, h):
        sc((buf, 1024 * h, 1024 * h + 1024), ("ind", ("xx", 0, NONE), ("nbo", 128 * d + 64 * h, 128 * d + 64 * h + 64)))
    gather("p3", 2, 1)
    weights("a3", 1, 1536, 512)
    gather("p2", 1, 1)
    gather("p3", 2, 0)
    prod("p1", 0, 0)
    prod("p1", 0, 1)
    cp(a("no"), a("nn"))
    tt(a("rho"), a("va2"), a("nn"), A.subtract)
    sa(a("rn"), a("nn"), 1, base)
    tt(a("v1", 0), a("rho"), a("v1", 1), A.mult)
    tt(a("rho"), a("nn"), a("v1", 0), A.add)
    cp(a("rhoo"), a("rho"))
    sa(("nx", NONE, EXT), ("rt", 0, 16), 0, 0)
    sc(("nx", 0, V), ("ind", ("hl", 0, V), ("no", 0, 128)))
    sc(("nxb", 0, 256), ("ind", ("nx", 0, V), ("blo", 0, 16)))
    send("6")
    alias("nx", "nxb")
    sa(("lw", 0, V), ("rt", 0, V), 0, -1)
    last = (1536, V)
    tt(("p3",) + last, ("p3",) + last, ("a0", 0, 512), A.mult)
    tt(("p2",) + last, ("p2",) + last, ("a3", 0, 512), A.mult)
    mm([(("v1", 0, 512), a("idf"), (p,) + last, p == "p1", p == "p3") for p in ("p1", "p2", "p3")])
    prod("p2", 1, 0)
    for lo, n, bank, w1 in ((0, 1024, "gw", None), (1024, 512, "v0", "a2")):
        acc = (bank, 0, n)
        tt(acc, ("p3", lo, lo + n), acc, A.mult)
        if w1:
            tt(("p2", lo, lo + n), ("p2", lo, lo + n), (w1, 0, n), A.mult)
        tt(acc, ("p2", lo, lo + n), acc, A.add)
        tt(("sx", lo, lo + n), ("p1", lo, lo + n), acc, A.add)
    sc(("sx",) + last, ("v1", 0, 512))
    sc(("sb", 0, 256), ("ind", ("sx", 0, V), ("blo", 0, 16)))
    send("5")
    alias("sx", "sb")
    sc(("p3", 0, 1024), ("sx", 0, 1024))
    sc(("gw", 0, 1024), ("sx", 1024, V))
    sa(("sx", NONE, NONE + 8), ("rt", 0, 8), 0, 0)
    sa(("sp", 0, 8), ("rt", 0, 8), 0, 0)
    tt(a("cmf"), a("rn"), a("rep"), A.mult)
    run("v", [("hl", 0, V)], [("ind", ("lw", 0, 2 * V), ("rhoo", 0, 128))],
        lambda: g.vector.tensor_copy(ap(("ind", ("lw", 0, 2 * V), ("rhoo", 0, 128))), T.hl[:, 0:V]))
    to_a("a3", 0, 128, "ehl", "lw")
    arrive("6")
    sc(("cg", 0, V), ("ind", ("nx", 0, EXT), ("lam", 0, 128)))
    to_a("a1", 0, 128, "ehl", "cg")
    arrive("5")
    sc(("p1", 1024, V), ("ind", ("sx", 0, NONE + 8), ("mo", 64, 128)))
    tt(("sp", 8, 1032), ("ind", ("sx", 0, NONE + 8), ("mo", 0, 64)), ("p3", 0, 1024), A.add)
    tt(("sp", 1032, V + 8), ("p1", 1024, V), ("gw", 0, 1024), A.add)
    ts(a("l1"), a("a3"), 8 - base, A.add, 0, A.max)
    for i in range(8):
        (sc if i % 2 else cp)(("yy", 256 * i, 256 * i + 256), ("ind", ("sp", 0, V + 8), ("l1", 16 * i, 16 * i + 16)))
    for i in range(8):
        dma("y", "y%d" % i, T.y[:, 256 * i:256 * i + 256], T.yy[:, 256 * i:256 * i + 256], [("yy", 256 * i, 256 * i + 256)], [])
    tt(a("cmf"), a("cmf"), a("a1"), A.add)
    dma("y", "cm", T.cm[:], T.cmf[:], [a("cmf")], [])
    need("g", [("loc", sent[0])] + [(s, count[s]) for s in ("v", "s", "t", "p")] + sorted(totals.items()))
